import numpy as np, ml_dtypes
CORES = [23,119,17,113]
N = 4
BF = ml_dtypes.bfloat16
W, I, B, S, RO, H = 4096, 128, 32, 6, 3, 9
def some(rng, k):
    o = np.argsort(rng.random(k.shape[:-1] + (16,) + k.shape[-1:]), axis=-2)
    return np.where(o < k[..., None, :], 0, 255)
def parts(rng):
    x = rng.integers(0, 256, (N, 8, 16, W)); w = rng.integers(0, 16, (N, 8, 16, 1)); c = rng.integers(0, 128, (N, 8, 16, I))
    l = rng.integers(1, 5, (N, 8, 16, I)); s = rng.integers(0, W, (N, 8, 16, I))
    v = rng.choice(np.array([96, 176, 208, 224, 236, 244, 252]), (N, 8, 1, I))
    return x, w, c, l, s, np.clip(v + rng.integers(-12, 13, (N, 8, 16, I)), 0, 255)
def small(a):
    return np.ascontiguousarray(a.reshape(N, 128, -1)).astype(np.float32).astype(BF)
def pack(x, w, c, l, s, fl):
    return {"x": small(x), "wt": small(w), "ch": small(c), "sp": small(l), "st": np.ascontiguousarray(s.reshape(N, 128, I)).astype(np.int32), "fl": small(fl)}
def setup_inputs(rng):
    return pack(*parts(rng))
def setup_inputs_spread(rng):
    x, w, c, l, s, fl = parts(rng)
    x = (np.exp2(8 * rng.random((N, 8, 1, W))) * rng.random(x.shape)).astype(np.int64)
    w = np.where(rng.random(w.shape) < 0.4, 0, w)
    c = np.where(rng.random((N, 8, 1, I)) < 0.5, c, np.exp2(7 * rng.random(c.shape)).astype(np.int64) - 1)
    l = rng.choice(np.array([1, 1, 1, 2, 3, 4]), l.shape)
    fl = (np.exp2(8 * rng.random((N, 8, 1, I))) * (0.5 + 0.5 * rng.random(fl.shape))).astype(np.int64)
    return pack(x, w, c, l, s, fl)
def setup_inputs_ends(rng):
    x, w, c, l, s, fl = parts(rng)
    d = rng.choice(np.array([0.04, 0.1, 0.3, 0.5]), (N, 8, 1, 1)); d[:, 7] = 0.5
    e = 255 * (rng.random(x.shape) < d); k = rng.random((N, 8, 1, W)); full = np.where(np.arange(8) == 7, 0.3, 0.03).reshape(1, 8, 1, 1)
    e = np.where(k < full, 255, np.where(k > 0.85, 0, e)); x = np.where((k > 0.5) & (k < 0.6), x, e)
    w = 15 * rng.integers(0, 2, w.shape); w[:, 7] = 15; w[:, 1] = 0; w[:, 0, 0] = 0; w[:, 0, 15] = 15
    b = rng.random((N, 8, 1, I)); c = np.where(b < 0.15, 127, np.where(b > 0.85, 0, 127 * rng.integers(0, 2, c.shape)))
    l = 1 + 3 * rng.integers(0, 2, l.shape); s = np.where(rng.random(s.shape) < 0.25, s, (W - 1) * rng.integers(0, 2, s.shape))
    fl = some(rng, rng.integers(0, 17, (N, 8, I))); fl[N - 2:] = some(rng, rng.integers(H, 17, (2, 8, I)))
    x[N - 2, 6, H - 1:] = 0; fl[N - 2, 6, :, I - 1] = np.where(np.arange(16) < H - 1, 0, 255)
    l[N - 1, 7, :, :2] = 4; s[N - 1, 7, :, :2] = W - 1
    l[N - 1, 7, 13:, I - 1] = np.array([1, 4, 4]); s[N - 1, 7, 13:, I - 1] = np.array([(0 - 613) & (W - 1), (W - 1 - 2452) & (W - 1), W - 1])
    c[N - 1, 7, 0, :2] = 127; c[N - 1, 7, 0, I - 1] = 127
    x[:, 7, :, (W - 1 + 2452) & (W - 1)] = 255; x[:, 7, :, W - 1] = 255; x[:, 7, 15] = 255
    return pack(x, w, c, l, s, fl)
def setup_inputs_corners(rng):
    x, w, c, l, s, fl = parts(rng); q = rng.permutation(N); ar = np.arange(16)[:, None]
    w[:, 0] = 0; b = rng.integers(0, 4, (N, 1, I)); c[:, 0] = np.where(b == 0, 3, np.where(b == 1, 0, np.where(b == 2, 127, c[:, 0])))
    x[:, 1] = np.minimum(x[:, 1], 254); fl[:, 1] = some(rng, rng.choice(np.array([0, H - 1, H, 16]), (N, I)))
    v = rng.integers(1, 255, (N, 16, 1)); x[:, 2] = v; fl[:, 2] = v + np.minimum(some(rng, rng.choice(np.array([H - 1, H, 16]), (N, I))), 1)
    w[:, 3] = 0; w[:, 3, 0] = 1; x[:, 3, 0, ::2] = 255; fl[:, 3] = fl[:, 3] // 2
    b = rng.integers(0, 4, (N, 1, I)); l[:, 4] = np.where(b == 0, 4, np.where(b == 1, 1, np.where(b == 2, 1 + 3 * (ar == 15), 1 + 3 * (ar & 1)))); fl[:, 4] = fl[:, 4] // 2
    e = (W - 1) * rng.integers(0, 2, (N, 16, I)); s[:, 5] = np.where(rng.random((N, 16, I)) < 0.5, e, (e - 613 * l[:, 5]) & (W - 1))
    w[:, 6] = 15; x[:, 6] = rng.integers(224, 256, (N, 16, W)); c[:, 6] = rng.choice(np.array([0, 126, 127]), (N, 16, I))
    x[q[0]] = np.minimum(x[q[0]], 254); fl[q[0]] = some(rng, np.full((8, I), H - 1))
    fl[q[1]] = some(rng, rng.integers(H, 17, (8, I))); fl[q[2]] = some(rng, rng.integers(H, 17, (8, I)))
    x[q[2], 7] = np.minimum(x[q[2], 7], 254); fl[q[2], 7, :, I - 1] = some(rng, np.full(1, H - 1))[:, 0]
    return pack(x, w, c, l, s, fl)
def setup_inputs_crowd(rng):
    x, w, c, l, s, fl = parts(rng); q = rng.permutation(N)
    s[:, :7] = rng.integers(0, W, (N, 7, 1, 1)); l[:, :7] = rng.integers(1, 5, (N, 7, 1, 1)); c[:, :7] = rng.integers(0, 128, (N, 7, 16, 1))
    s[:, 4:7, 15, I - 1] = rng.integers(0, W, (N, 3)); c[:, 4:7, :, I - 1] = rng.integers(0, 128, (N, 3, 16))
    fl = some(rng, rng.integers(H, 17, (N, 8, I)))
    for a in q[:N // 2]:
        x[a, 7] = np.minimum(x[a, 7], 254); fl[a, 7, :, I - 1] = some(rng, np.full(1, H - 1))[:, 0]
    return pack(x, w, c, l, s, fl)
def setup_inputs_late(rng):
    x, w, c, l, s, fl = parts(rng); q = rng.permutation(N); a, b = int(q[0]), int(q[1])
    x[a] = np.minimum(x[a], 254); fl[a] = some(rng, np.full((8, I), H - 1)); fl[b] = some(rng, rng.integers(H, 17, (8, I)))
    for r, g, low in ((a, 7, 8), (b, 0, 0)):
        hot = B * int(rng.integers(8, I)); w[r, g] = 0
        x[r, g] = rng.integers(0, 101, (16, W)); x[r, g, :, hot] = rng.integers(200, 255, 16)
        fl[r, g, :, low:] = rng.integers(110, 151, (16, I - low))
        l[r, g] = 1; s[r, g] = (hot - 613) & (W - 1)
        if g == 7: l[(a - 2) % N, 7] = 1; s[(a - 2) % N, 7] = (hot - 613) & (W - 1)
    s[(a - 1) % N, 7] = (16 * rng.integers(0, W // 16, (16, I)) - (I - 8)) & (W - 1)
    l[(b - 1) % N, 0] = 1; s[(b - 1) % N, 0] = W - 613 - 8 * I
    c[(b - 1) % N, 0] = 16 * rng.integers(0, 8, (16, I)) + 4 * rng.integers(1, 4, (16, I))
    return pack(x, w, c, l, s, fl)
def check_inputs(d):
    bad = []
    for k, lo, hi in (("x", 0, 255), ("wt", 0, 15), ("ch", 0, 127), ("sp", 1, 4), ("st", 0, W - 1), ("fl", 0, 255)):
        v = np.asarray(d[k]).astype(np.float64)
        if not (np.all(v >= lo) and np.all(v <= hi)): bad.append("range of " + k)
        if np.any(v != np.floor(v)): bad.append("whole numbers of " + k)
    return bad
def reference(x, wt, ch, sp, st, fl):
    X, Q, C, L, Z, F = [v.astype(np.float32).astype(np.int32).reshape(N, 8, 16, -1) for v in (x, wt, ch, sp, st, fl)]
    A = [0] * N; row = np.arange(16)[:, None]
    for t in range(RO):
        if t > 0: C, L, Z = np.roll(C, 1, axis=0), np.roll(L, 1, axis=0), np.roll(Z, 1, axis=0)
        for a in range(N):
            l = L[a]
            at = np.arange(16)[None, :, None, None]; at = at + np.where(at >= row[None, None], l[:, None], 0)
            e = np.take_along_axis(np.concatenate([C[a], np.zeros((8, 4, I), np.int32)], axis=1)[:, :, None, :], at, 1)
            e = np.concatenate([e, np.zeros((8, 1, 16, I), np.int32)], axis=1)
            s = (Z[a] + 613 * l + A[a]) & (W - 1); p = np.zeros((8, 16, I), np.int64); V = np.zeros((8, 16, 16, I), np.int32); log = []
            for k in range(S):
                z = np.take_along_axis(X[a], s.reshape(8, 1, 16 * I), 2).reshape(8, 16, 16, I)
                V = np.maximum(V, z); c = np.take_along_axis(e, np.minimum(p, 16)[:, None], 1)[:, 0].astype(np.int64)
                u = np.add.reduce(Q[a][..., None] * z, axis=1).astype(np.int64)
                n = 1 + (((u >> 3) + c) & 3); log.append((p, n))
                s = (((u * (2 * c + 1)) >> 3) + 37 * u + c) & (W - 1); p = p + n
            fails = np.add.reduce((V >= F[a][:, :, None, :]).astype(np.int32), axis=1) >= H
            best = np.argmax(np.where(fails, 16 * l + 15 - row[None], 0 - 1), axis=1)[:, None, :]; ok = np.any(fails, axis=1)[:, None, :]
            nl = np.ones((8, 16, I), np.int64)
            for p, n in log: nl = np.where(row[None] == np.take_along_axis(p, best, 1), np.take_along_axis(n, best, 1), nl)
            v = np.take_along_axis(V, best[:, None], 2)[:, :, 0]
            C[a] = np.where(ok, np.take_along_axis(e[:, :16], best[:, None], 2)[:, :, 0], C[a]); L[a] = np.where(ok, nl, l)
            to = B * np.arange(I)[None, None, :] + (np.add.reduce(Q[a] * v, axis=1)[:, None, :] & (B - 1))
            to = np.broadcast_to(to, (8, 16, I)); np.put_along_axis(X[a], to, np.where(ok, v, np.take_along_axis(X[a], to, 2)), 2)
            F[a] = np.where(ok, (F[a] + v) >> 1, F[a]); A[a] = int(np.sum(ok))
    sums = np.add.reduce(X.reshape(N, 128, I, B), axis=3)
    return {"yc": C.reshape(N, 128, I).astype(np.float32).astype(BF), "yl": L.reshape(N, 128, I).astype(np.float32).astype(BF),
            "yf": F.reshape(N, 128, I).astype(np.float32).astype(BF), "ys": sums.astype(np.float32)}

@@ -1,0 +1,532 @@
+import numpy as np
+from concourse.mybir import dt, AluOpType as O, AxisListType, ActivationFunctionType as AF
+
+H2 = 64
+NV = {"A": 4, "B": 10}
+EQS = {"A": 1, "B": 0}
+LV = {"A": (1,), "B": (1, 2)}
+TILE = (1, 1, 2, 3, 3, 3)
+WID = {1: 10, 2: 12, 3: 15}
+RR = {1: list(range(8, -1, -1)), 2: list(range(12, 2, -1)) + [17], 3: list(range(16, 3, -1)) + [18]}
+SCRATCH = {}
+SEMAPHORES = ["sv", "ss", "st_", "sg", "loc", "arst1", "arst2"] + ["arr%d%s%s" % (t, x, h) for t in (1, 2) for x in "LC" for h in "AB"]
+SEMAPHORES += ["d%d" % k for k in range(16)]
+_BF, _F32, _I32 = "bfloat16", "float32", "int32"
+for _n, _c, _d in (("X", 4096 + 128, _BF), ("chs", 128, _BF), ("sps", 128, _BF), ("fls", 128, _BF), ("wts", 1, _BF), ("stI", 128, _I32),
+                   ("st16", 128, "uint16"), ("stin1", 128, "uint16"), ("stin2", 128, "uint16"), ("pI", 1, _I32), ("aI", 1, _I32),
+                   ("qc", 1, _F32), ("qk", 6, _F32), ("nq", 6, _F32), ("iz", 1, _F32), ("q6", 1, _F32), ("q16", 1, _F32), ("m15", 1, _F32),
+                   ("ones", 128, _BF), ("bm0", 128, _BF), ("bm", 128, _BF), ("nbm", 128, _BF), ("idn", 128, _BF), ("nid", 128, _BF),
+                   ("tri", 128, _BF), ("shm", 512, _BF), ("hsd", 512, _BF), ("hsh", 512, _BF), ("hid", 256, _BF), ("kc", 128, _BF),
+                   ("thr", 4, _F32), ("half", 5, _F32), ("onec", 1, _F32), ("g8", 8, _F32), ("g8w", 8, _F32), ("Wm", 2048, _BF), ("Em", 2048, _BF),
+                   ("jrow", 18, _F32), ("cqx", 18, _F32), ("dif", 17, _F32), ("dif8", 19, _F32), ("Rm", 19 * 128, _BF), ("il0", 4, _F32),
+                   ("il", 4, _F32), ("m6", 1536, _BF), ("m16", 128, _BF)):
+    SCRATCH[_n] = ("sbuf", [128, _c], _d)
+_PACK = {}
+_SMALL = {_BF: (("w", 64), ("b", 64), ("key", 64), ("fk", 64), ("Kp", 64), ("bT", 64), ("okS", 64), ("aL", 64), ("aM", 64), ("acc", 64),
+                ("nok", 64), ("nokL", 64), ("Vsel", 64), ("xo", 64), ("yfs", 64), ("Fs", 64), ("kb", 128)),
+          _F32: (("stf", 64), ("sta", 64), ("tt", 4), ("fd", 64), ("asum", 1), ("K1", 4), ("K2", 4), ("Kv", 4), ("S0", 64), ("yss", 64),
+                 ("base", 64), ("xd", 64), ("xe", 64), ("t1", 64)),
+          _I32: (("n1", 64), ("k8", 64), ("h0", 4), ("h1", 4), ("h2", 4), ("h3", 4), ("fi", 64), ("s0", 64), ("s1", 64), ("t2", 64), ("t4", 64), ("t5", 64))}
+for _h in "AB":
+    for _d, _names in _SMALL.items():
+        _at = 0
+        for _n, _c in _names:
+            _PACK[_n + _h] = ("pk" + _d[0] + _h, _at, _c)
+            _at += -(-_c // 32) * 32
+        SCRATCH["pk" + _d[0] + _h] = ("sbuf", [128, _at], _d)
+    for _n, _c, _d in (("z", 6144, _BF), ("VS", 6144, _BF), ("ind", 1024, _BF), ("off", 64, "uint16"), ("mk", 960, _BF), ("co", 960, _BF),
+                       ("AP", 448, _BF), ("ES", 256, _BF), ("EC", 256, _BF), ("EQ", 384, _BF), ("EN", 384, _BF), ("SQ", 320, _BF),
+                       ("voff", 4, "uint16"), ("toff", 4, "uint16")):
+        SCRATCH[_n + _h] = ("sbuf", [128, _c], _d)
+    for _q in (1, 2, 3):
+        for _n in ("L", "da", "db"):
+            SCRATCH["%s%d%s" % (_n, _q, _h)] = ("sbuf", [128, 64 * WID[_q]], _BF)
+    for _x in "LC":
+        for _t in (0, 1, 2):
+            SCRATCH["s%d%s%s" % (_t, _x, _h)] = ("sbuf", [128, 64], _BF)
+        for _t in (1, 2):
+            SCRATCH["in%d%s%s" % (_t, _x, _h)] = ("sbuf", [128, 64], _BF)
+    for _n in ("pU", "p37", "pV", "pM"):
+        SCRATCH[_n + _h] = ("psum", [128, 512], _F32)
+
+
+def rank_program(g, core, T, topo):
+    rank = T.rank_of(core)
+    if rank is None:
+        return
+    N = len(T.cores)
+    eng = {"v": g.vector, "s": g.scalar, "t": g.tensor, "y": g.sync, "g": g}
+    qsem = {"v": "sv", "s": "ss", "t": "st_", "g": "sg"}
+    CV, CS, CT = 0.00083 * 1.2, 0.00083 * 1.2, 0.00083 * 0.85
+    GATH = 0.07 + 1024 * 1.56 * CS
+    ops = []
+    lastw, readers, bank = {}, {}, {}
+    ndma, loc = [0], [0]
+
+    def B(name, a=0, b=None, step=1):
+        big, at, c = _PACK[name] if name in _PACK else (name, 0, SCRATCH[name][1][1])
+        e = c if b is None else b
+        return T[big][:, at + a:at + e:step] if step != 1 else T[big][:, at + a:at + e]
+
+    def add(q, cost, fns, r=(), w=(), banks=(), sem=None, extra=(), after=()):
+        k = len(ops)
+        deps = set(extra)
+        for x in r:
+            if x in lastw:
+                deps.add(lastw[x])
+            readers.setdefault(x, []).append(k)
+        for x in w:
+            if x in lastw:
+                deps.add(lastw[x])
+            deps.update(readers.get(x, ()))
+            lastw[x] = k
+            readers[x] = []
+        for x in banks:
+            st = bank.setdefault(x, [None, [], []])
+            if st[0] != q:
+                st[0], st[1], st[2] = q, st[2], []
+            deps.update(st[1])
+            st[2].append(k)
+        deps.discard(k)
+        ops.append({"q": q, "cost": cost, "fns": fns, "deps": deps, "all": deps | set(after), "sem": sem})
+        return k
+
+    def V(n, fn, r, w, banks=(), **kw):
+        return add("v", max(64, n) * CV, [fn], r, w, banks, **kw)
+
+    def S(n, fn, r, w, banks=()):
+        return add("s", 0.03 + max(40, n) * CS, [fn], r, w, banks)
+
+    def P(cols, fns, r, w, banks=(), **kw):
+        return add("t", 0.02 + cols * CT, fns, r, w, banks, **kw)
+
+    def TS(out, in0, s1, s2, o0, o1=None):
+        if o1 is None:
+            return lambda: g.vector.tensor_scalar(out, in0, s1, None, o0)
+        return lambda: g.vector.tensor_scalar(out, in0, s1, s2, o0, o1)
+
+    def TT(out, a, b, op):
+        return lambda: g.vector.tensor_tensor(out, a, b, op)
+
+    def CP(out, a):
+        return lambda: g.vector.tensor_copy(out, a)
+
+    def MS(ap, c):
+        return lambda: g.vector.memset(ap, c)
+
+    def SCAN(out, d0, d1, o0, o1):
+        return lambda: g.vector.tensor_tensor_scan(out, d0, d1, 0.0, o0, o1)
+
+    def ACT(out, in_, f, **kw):
+        return lambda: g.scalar.activation(out, in_, f, **kw)
+
+    def MM(out, l, r, a, z):
+        return lambda: g.tensor.matmul(out, l, r, a, z)
+
+    def dma(q, out, in_, r, w, cost=2.2):
+        s = "d%d" % ndma[0]
+        ndma[0] += 1
+        return add(q, cost, [lambda: eng[q].dma_start(out, in_)], r, w, sem=(s, 16))
+
+    def aff(out, in_, pat, cmp, base, cm, r, w):
+        return add("g", 0.4, [lambda: g.affine_select(out, in_, pat, cmp, 0.0, base, cm)], r, w)
+
+    NE = min(len(topo.engines(core, c)) for c in T.cores if c != core)
+
+    def send(name_in, name_out, sem, hop, r):
+        dst = T.cores[(rank + hop) % N]
+        rid, pid = topo.addr(dst)[:2]
+        lanes = sum(1 << e for e in topo.engines(core, dst)[:NE])
+        loc[0] += NE
+        k = add("g", 0.3, [lambda: g.remote_dma(T[name_out][:], T[name_in][:], T.sem[sem], T.sem.loc, pid, rid, lanes)], r, (), sem=("loc", None))
+        return add("r", 2.5, [], (), (name_out,), sem=(sem, NE), extra=(k,))
+
+    dma("s", T.stI[:], T.st[:], (), ("stI",))
+    dma("y", T.sps[:], T.sp[:], (), ("sps",))
+    dma("y", T.X[:, 0:4096], T.x[:], (), ("X",), 6.0)
+    dma("s", T.wts[:], T.wt[:], (), ("wts",))
+    dma("s", T.chs[:], T.ch[:], (), ("chs",))
+    dma("s", T.fls[:], T.fl[:], (), ("fls",))
+    V(64, MS(T.X[:, 4096:4224], 0.0), (), ("Xd",))
+    V(128, CP(T.st16[:], T.stI[:]), ("stI",), ("st16",))
+    send("st16", "stin1", "arst1", 1, ("st16",))
+    send("st16", "stin2", "arst2", 2, ("st16",))
+    add("g", 0.2, [lambda: g.iota(T.pI[:], [[0, 1]], 0, 1)], (), ("pI",))
+    add("g", 0.2, [lambda: g.iota(T.jrow[:], [[1, 18]], -1, 0, allow_small_or_imprecise_dtypes=True)], (), ("jrow",))
+    add("g", 0.2, [lambda: g.iota(T.il0[:], [[16, 4]], 0, 0, allow_small_or_imprecise_dtypes=True)], (), ("il0",))
+    V(64, MS(T.ones[:], 1.0), (), ("ones",))
+    V(1, TS(T.aI[:], T.pI[:], 15, None, O.bitwise_and), ("pI",), ("aI",))
+    V(1, CP(T.qc[:], T.aI[:]), ("aI",), ("qc",))
+    for k in range(6):
+        V(1, TS(T.qk[:, k:k + 1], T.qc[:], float(-k), None, O.add), ("qc",), ("qk%d" % k,))
+    V(1, MS(T.onec[:], 1.0), (), ("onec",))
+    for l in range(5):
+        V(1, MS(T.half[:, l:l + 1], 0.5 - l), (), ("half%d" % l,))
+    V(1, TS(T.iz[:], T.qc[:], 0.0, None, O.is_equal), ("qc",), ("iz",))
+    V(1, TS(T.m15[:], T.qc[:], 15.0, None, O.is_equal), ("qc",), ("m15",))
+    V(1, TS(T.q6[:], T.qc[:], 6.0, None, O.mult), ("qc",), ("q6",))
+    V(1, TS(T.q16[:], T.qc[:], -1.0, 16.0, O.mult, O.add), ("qc",), ("q16",))
+    V(6, TS(T.nq[:], T.qk[:], -1.0, None, O.mult), tuple("qk%d" % k for k in range(6)), ("nq",))
+    aff(T.bm0[:], T.ones[:], [[-16, 8], [0, 16]], O.is_ge, 0, 1, ("ones",), ("bm0",))
+    aff(T.bm[:], T.bm0[:], [[16, 8], [0, 16]], O.is_ge, 15, -1, ("bm0",), ("bm",))
+    aff(T.idn[:], T.ones[:], [[-1, 128]], O.is_equal, 0, 1, ("ones",), ("idn",))
+    V(4, TS(T.il[:], T.il0[:], T.qc[:], None, O.add), ("il0", "qc"), ("il",))
+    V(18, TS(T.cqx[:], T.jrow[:], T.qc[:], None, O.is_equal), ("jrow", "qc"), ("cqx",))
+    V(17, TT(T.dif[:], T.cqx[:, 1:18], T.cqx[:, 0:17], O.subtract), ("cqx",), ("dif",))
+    V(17, TS(T.dif8[:, 0:17], T.dif[:], 8.0, None, O.mult), ("dif",), ("dif8a",))
+    V(2, TS(T.dif8[:, 17:19], T.cqx[:, 3:5], 8.0, None, O.mult), ("cqx",), ("dif8b",))
+    for r in list(range(8, -1, -1)) + [17, 18] + list(range(16, 8, -1)):
+        tok = ("bm", "dif8b" if r > 16 else "dif8a")
+        if r < 9:
+            V(64, TS(T.Rm[:, r * 128:(r + 1) * 128], T.bm[:], T.dif8[:, r:r + 1], None, O.mult), tok, ("Rm%d" % r,))
+        else:
+            S(128, ACT(T.Rm[:, r * 128:(r + 1) * 128], T.bm[:], AF.Copy, scale=T.dif8[:, r:r + 1]), tok, ("Rm%d" % r,))
+    V(8, CP(T.g8[:], T.bm[:, 0::16]), ("bm",), ("g8",))
+    V(8, TS(T.g8w[:], T.g8[:], T.wts[:], None, O.mult), ("g8", "wts"), ("g8w",))
+    V(1024, MS(T.Wm[:], 0.0), (), ("Wz",))
+    V(1024, MS(T.Em[:], 0.0), (), ("Ez",))
+    for gg in range(8):
+        sl = slice(16 * gg, 16 * gg + 15 * 129 + 1, 129)
+        S(16, ACT(T.Wm[:, sl], T.ones[:, 0:16], AF.Copy, scale=T.g8w[:, gg:gg + 1]), ("g8w", "Wz", "ones"), ("Wm%d" % gg,))
+    for gg in range(8):
+        sl = slice(16 * gg, 16 * gg + 15 * 129 + 1, 129)
+        S(16, ACT(T.Em[:, sl], T.ones[:, 0:16], AF.Copy, scale=T.g8[:, gg:gg + 1]), ("g8", "Ez", "ones"), ("Em%d" % gg,))
+    EM = tuple("Em%d" % m for m in range(8))
+    WM = tuple("Wm%d" % m for m in range(8))
+    V(64, MS(T.kc[0:64, :], -512.0), (), ("kc0",))
+    V(64, MS(T.kc[64:128, :], 0.0625), (), ("kc1",))
+    V(64, TS(T.nid[:], T.idn[:], -1.0, None, O.mult), ("idn",), ("nid",))
+    V(64, TS(T.nbm[:], T.bm[:], -1.0, None, O.mult), ("bm",), ("nbm",))
+    aff(T.tri[:], T.bm[:], [[1, 128]], O.is_ge, 0, -1, ("bm",), ("tri",))
+    for l in range(1, 5):
+        aff(T.shm[:, (l - 1) * 128:l * 128], T.bm[:], [[-1, 128]], O.is_equal, -l, 1, ("bm",), ("shm%d" % l,))
+    for l in range(1, 5):
+        V(256, TT(T.hsd[:, (l - 1) * 128:l * 128], T.shm[:, (l - 1) * 128:l * 128],
+                  T.idn[:] if l == 1 else T.shm[:, (l - 2) * 128:(l - 1) * 128], O.subtract),
+          ("shm%d" % l, "idn" if l == 1 else "shm%d" % (l - 1)), ("hsd%d" % l,))
+    V(256, TS(T.hsh[:], T.hsd[:], 0.5, None, O.mult), ("hsd1", "hsd2", "hsd3", "hsd4"), ("hsh",))
+    V(64, TS(T.hid[:, 0:128], T.idn[:], 0.5, None, O.mult), ("idn",), ("hid0",))
+    V(64, TS(T.hid[:, 128:256], T.shm[:, 384:512], 0.5, None, O.mult), ("shm4",), ("hid1",))
+    V(768, MS(T.m6[:], 1.0), (), ("m6",))
+    V(256, MS(T.m6[:, 0::6], 0.0), (), ("m6",))
+    V(64, MS(T.m16[:], 1.0), (), ("m16",))
+    V(8, MS(T.m16[:, 0::16], 0.0), (), ("m16",))
+    for hi, h in enumerate("AB"):
+        for q in (1, 2, 3):
+            n = WID[q]
+            a, b, l = ("%s%d%s" % (x, q, h) for x in ("da", "db", "L"))
+            for x in (a, b):
+                if q == 1:
+                    V(n * 32, MS(T[x][:], 1.0), (), (x,))
+                else:
+                    add("g", 0.13 + n * 128 * CS, [lambda x_=T[x], n_=n: g.iota(x_[:], [[0, 64 * n_]], 1, 0, allow_small_or_imprecise_dtypes=True)], (), (x,))
+            S(64, ACT(T[a][:, 0::n], T.ones[:, 0:64], AF.Copy, scale=64.0), ("ones",), (a,))
+            S(64, ACT(T[b][:, 1::n], T.ones[:, 0:64], AF.Copy, scale=0.0), ("ones",), (b,))
+            S(64, ACT(T[l][:, 0::n], T.ones[:, 0:64], AF.Copy, scale=0.0), ("ones",), (l + "z",))
+        V(4, TS(B("K1" + h), T.il[:], 31.0, float(31 * H2 * hi - 4096), O.mult, O.add), ("il",), ("K1" + h,))
+        V(4, TS(B("K2" + h), T.il[:], float(4096 + H2 * hi), None, O.add), ("il",), ("K2" + h,))
+        V(4, TS(B("Kv" + h), T.il[:], 96.0, 5.0, O.mult, O.add), ("il",), ("Kv" + h,))
+        V(64, MS(T["AP" + h][:, 0:64], 0.0), (), ("AP0" + h,))
+        V(64, TS(T["EQ" + h][:, 0:64], T.ones[:, 0:64], T.iz[:], None, O.mult), ("ones", "iz"), ("EQ0" + h,))
+        V(1, MS(B("asum" + h), 0.0), (), ("asum" + h,))
+        V(64, CP(T["pV" + h][:, 448:512], T.fls[:, H2 * hi:H2 * hi + H2]), ("fls",), ("F" + h,), ("pV" + h,))
+        V(64, CP(B("Fs" + h), T.fls[:, H2 * hi:H2 * hi + H2]), ("fls",), ("Fs" + h,))
+        V(64, TS(T.thr[:, hi:hi + 1], T.qc[:], NV[h] - 0.5, None, O.is_ge), ("qc",), ("thr0" + h,))
+        V(64, TS(T.thr[:, 2 + hi:3 + hi], T.thr[:, hi:hi + 1], -7.5, 8.5, O.mult, O.add), ("thr0" + h,), ("thr" + h,))
+
+    def rec(t, h):
+        o = H2 * "AB".index(h)
+        if t == 0:
+            return T.chs[:, o:o + H2], T.sps[:, o:o + H2], "chs", "sps"
+        c, l = "in%dC%s" % (t, h), "in%dL%s" % (t, h)
+        return T[c][:], T[l][:], c, l
+
+    def vm(h, m):
+        return T["VS" + h][:, 6 * m + 5::96]
+
+    def entry(k, h):
+        q = TILE[k]
+        n = WID[q]
+        L = "L%d%s" % (q, h)
+        V(n * 32, SCAN(T["mk" + h][:, 0:64 * n], T["da%d%s" % (q, h)][:], T["db%d%s" % (q, h)][:], O.add, O.min),
+          ("da%d%s" % (q, h), "db%d%s" % (q, h)), ("mk" + h,))
+        V(n * 32, SCAN(T["co" + h][:, 0:64 * n], T["mk" + h][:, 0:64 * n], T[L][:], O.mult, O.add),
+          ("mk" + h, L + "z") + tuple("%s_%d" % (L, r) for r in RR[q]), ("co" + h,))
+        if k < 5:
+            V(64, TS(B("w" + h), T["co" + h][:, n - 1:64 * n:n], 0.25, 2.0, O.mult, O.add), ("co" + h,), ("w" + h,))
+
+    for t in range(3):
+        last = t == 2
+        for hi, h in enumerate("AB"):
+            C, L, ct, lt = rec(t, h)
+            pV, pM, pU, p37 = T["pV" + h], T["pM" + h], T["pU" + h], T["p37" + h]
+            o = H2 * hi
+            src, stt = ((T.stI, "stI"), (T.stin1, "stin1"), (T.stin2, "stin2"))[t]
+            V(64, CP(B("stf" + h), src[:, o:o + H2]), (stt,), ("stf" + h,))
+            V(64, TS(B("sta" + h), B("stf" + h), B("asumA"), B("asumB"), O.add, O.add), ("stf" + h, "asumA", "asumB"), ("sta" + h,))
+            V(64, TS(B("base" + h), L, 613.0, None, O.mult), (lt,), ("base" + h,))
+            V(128, TT(B("s0" + h), B("base" + h), B("sta" + h), O.add), ("base" + h, "sta" + h), ("s0" + h,))
+            V(64, TS(B("s1" + h), B("s0" + h), 4095, None, O.bitwise_and), ("s0" + h,), ("s1" + h,))
+            V(64, CP(T["off" + h][:], B("s1" + h)), ("s1" + h,), ("off" + h,))
+            V(64, CP(pV[:, 384:448], L), (lt,), ("L" + h,), ("pV" + h,))
+            S(64, ACT(B("Kp" + h), L, AF.Identity, scale=16.0, bias=T.q16[:]), (lt, "q16"), ("Kp" + h,))
+            S(64, ACT(T["da1" + h][:, 1::10], L, AF.Copy, scale=T.iz[:]), (lt, "iz"), ("da1" + h,))
+            S(64, ACT(T["db1" + h][:, 0::10], T.ones[:, 0:64], AF.Copy, scale=-8.0), ("ones",), ("db1" + h,))
+            P(512, [MM(pM[:, 64 * j:64 * j + 64], T.Rm[:, (8 - j) * 128:(9 - j) * 128], C, True, True) for j in range(8)],
+              (ct,) + tuple("Rm%d" % (8 - j) for j in range(8)), ("dM" + h,), ("pM" + h,))
+            P(192, [MM(pU[:, 64 * j:64 * j + 64], T.Rm[:, r * 128:(r + 1) * 128], C, True, True) for j, r in enumerate((0, 17, 18))],
+              (ct, "Rm0", "Rm17", "Rm18"), ("dU" + h,), ("pU" + h,))
+            P(512, [MM(p37[:, 64 * j:64 * j + 64], T.Rm[:, (16 - j) * 128:(17 - j) * 128], C, True, True) for j in range(8)],
+              (ct,) + tuple("Rm%d" % (16 - j) for j in range(8)), ("d37" + h,), ("p37" + h,))
+            at = {r: (pM, 8 - r, "dM" + h, "pM" + h) for r in range(1, 9)}
+            at.update({r: (p37, 16 - r, "d37" + h, "p37" + h) for r in range(9, 17)})
+            at.update({r: (pU, j, "dU" + h, "pU" + h) for j, r in enumerate((0, 17, 18))})
+            for q in (1, 2, 3):
+                n = WID[q]
+                todo = list(enumerate(RR[q]))
+                for j, r in (todo if q == 1 else todo[::-1]):
+                    ps, jj, tk, bk = at[r]
+                    out, in_ = T["L%d%s" % (q, h)][:, 1 + j::n], ps[:, 64 * jj:64 * jj + 64]
+                    low = r in (0, 17, 18)
+                    if q in LV[h]:
+                        V(64, TS(out, in_, -4.0, None, O.add) if low else CP(out, in_), (tk,), ("L%d%s_%d" % (q, h, r),), (bk,))
+                    else:
+                        S(64, ACT(out, in_, AF.Copy, bias=-4.0) if low else ACT(out, in_, AF.Copy), (tk,), ("L%d%s_%d" % (q, h, r),), (bk,))
+            entry(0, h)
+        for k in range(6):
+            for h in "AB":
+                pV, pU = T["pV" + h], T["pU" + h]
+                n = WID[TILE[k]]
+                c8 = T["co" + h][:, n - 1:64 * n:n]
+                zk, z = "z%d%s" % (k, h), T["z" + h]
+                add("s", GATH, [lambda o_=z[:, k::6], f_=T["off" + h]: g.scalar.activation(o_, T.X[:, 0:4096].indirect(f_[:, 0:64]), AF.Copy)],
+                    ("X", "off" + h), (zk,))
+                P(17 * 64, [MM(pU[:, 0:64], T.kc[:], T.ones[:, 0:64], True, False)]
+                  + [MM(pU[:, 0:64], T.Wm[:, 128 * m:128 * m + 128], z[:, 6 * m + k::96], False, m == 15) for m in range(16)],
+                  (zk, "kc0", "kc1", "ones") + WM, ("u" + h,), ("pU" + h,))
+                y4 = pU[:, 0:64]
+                if k < 5:
+                    V(64, TT(B("t1" + h), y4, B("w" + h), O.mult), ("u" + h, "w" + h), ("t1" + h,), ("pU" + h,))
+                    V(64, TS(pU[:, 64:128], y4, 37.0, -148.0, O.mult, O.add), ("u" + h,), ("t3" + h,), ("pU" + h,))
+                    V(64, TS(B("t2" + h), B("t1" + h), 0.125, -0.9375, O.mult, O.add), ("t1" + h,), ("t2" + h,))
+                    V(64, TT(B("t4" + h), B("t2" + h), pU[:, 64:128], O.add), ("t2" + h, "t3" + h), ("t4" + h,), ("pU" + h,))
+                    V(64, TS(B("t5" + h), B("t4" + h), 4095, None, O.bitwise_and), ("t4" + h,), ("t5" + h,))
+                    V(64, CP(T["off" + h][:], B("t5" + h)), ("t5" + h,), ("off" + h,))
+                V(64, TT(B("k8" + h), y4, c8, O.add), ("u" + h, "co" + h), ("k8" + h,), ("pU" + h,))
+                V(64, TS(B("n1" + h), B("k8" + h), 3, 3, O.arith_shift_right, O.bitwise_and), ("k8" + h,), ("n1" + h,))
+                Pk, pt = pV[:, 64 * k:64 * k + 64], "P%d%s" % (k + 1, h)
+                if k == 0:
+                    V(64, CP(Pk, B("n1" + h)), ("n1" + h,), (pt,), ("pV" + h,))
+                else:
+                    V(64, TT(Pk, B("n1" + h), pV[:, 64 * k - 64:64 * k], O.add), ("n1" + h, "P%d%s" % (k, h)), (pt,), ("pV" + h,))
+                if k < 5:
+                    q = TILE[k + 1]
+                    n2, da, db = WID[q], "da%d%s" % (q, h), "db%d%s" % (q, h)
+                    V(64, TS(T[db][:, 0::n2], Pk, float(k + 1 - RR[q][0]), None, O.add), (pt,), (db,), ("pV" + h,))
+                    V(64, TS(B("b" + h), Pk, T.qk[:, k + 1:k + 2], None, O.is_ge), (pt, "qk%d" % (k + 1)), ("b" + h,), ("pV" + h,))
+                    V(64, TT(T[da][:, 1::n2], B("b" + h), pV[:, 384:448], O.mult), ("b" + h, "L" + h), (da,), ("pV" + h,))
+                    entry(k + 1, h)
+        if last:
+            for hi, h in enumerate("AB"):
+                pM = T["pM" + h]
+                P(2048, [MM(pM[:, 0:64], T.idn[:], T.X[:, 2048 * hi + j:2048 * hi + 2048:32], j == 0, j == 31) for j in range(32)],
+                  ("X", "idn"), ("sums" + h,), ("pM" + h,))
+                V(64, CP(B("S0" + h), pM[:, 0:64]), ("sums" + h,), ("S0" + h,), ("pM" + h,))
+        for hi, h in enumerate("AB"):
+            C, L, ct, lt = rec(t, h)
+            pV, pM, pU, p37 = T["pV" + h], T["pM" + h], T["pU" + h], T["p37" + h]
+            tbn = "pUA" if h == "A" else "pMA"
+            tb = T[tbn]
+            o = H2 * hi
+            sL, sC = "s%dL%s" % (t, h), "s%dC%s" % (t, h)
+            for j in range(4):
+                sl = slice(1536 * j, 1536 * j + 1536)
+                V(768, SCAN(T["VS" + h][:, sl], T.m6[:], T["z" + h][:, sl], O.mult, O.max), tuple("z%d%s" % (k, h) for k in range(6)) + ("m6",), ("VS%d%s" % (j, h),))
+            vt = tuple("VS%d%s" % (j, h) for j in range(4))
+            for c, m0 in enumerate(range(NV[h], 16, 8)):
+                ms = range(m0, min(16, m0 + 8))
+                ps, bk = (p37, "p37" + h) if c == 0 else (pM, "pM" + h)
+                mm = []
+                for j, m in enumerate(ms):
+                    mm += [MM(ps[:, 64 * j:64 * j + 64], T.idn[:], vm(h, m), True, False), MM(ps[:, 64 * j:64 * j + 64], T.nid[:], B("Fs" + h), False, True)]
+                P(128 * len(ms), mm, vt + ("Fs" + h, "idn", "nid"), ("VF%d%s" % (c, h),), (bk,))
+                S(64 * len(ms), ACT(T["ind" + h][:, 64 * m0:64 * (m0 + len(ms))], ps[:, 0:64 * len(ms)], AF.Sign, bias=T.half[:, 0:1]),
+                  ("VF%d%s" % (c, h), "half0"), tuple("ind%d%s" % (m, h) for m in ms), (bk,))
+            for m in range(NV[h]):
+                V(64, TT(T["ind" + h][:, 64 * m:64 * m + 64], vm(h, m), pV[:, 448:512], O.is_ge), vt + ("F" + h,), ("ind%d%s" % (m, h),), ("pV" + h,))
+            prev = ()
+            for c in range(2):
+                prev = (P(512, [MM(pU[:, 0:64], T.Em[:, 128 * m:128 * m + 128], T["ind" + h][:, 64 * m:64 * m + 64], m == 0, m == 15) for m in range(8 * c, 8 * c + 8)],
+                          tuple("ind%d%s" % (m, h) for m in range(8 * c, 8 * c + 8)) + EM, ("cnt%d%s" % (c, h),), ("pU" + h,), after=prev),)
+            V(64, TS(B("fk" + h), pU[:, 0:64], T.thr[:, 2 + hi:3 + hi], None, O.is_ge), ("cnt0" + h, "cnt1" + h, "thr" + h), ("fk" + h,), ("pU" + h,))
+            V(128, TT(B("key" + h), B("fk" + h), B("Kp" + h), O.mult), ("fk" + h, "Kp" + h), ("key" + h,))
+            big, kat, _ = _PACK["kb" + h]
+            kb = T[big][0:64, kat:kat + 128]
+            P(128, [MM(pM[0:64, 0:128], B("key" + h), T.idn[:], True, True)], ("key" + h, "idn"), ("kT" + h,), ("pM" + h,))
+            V(128, SCAN(kb, T.m16[0:64, :], pM[0:64, 0:128], O.mult, O.max), ("kT" + h, "m16"), ("kb" + h,), ("pM" + h,))
+            P(64, [MM(pM[:, 128:192], kb, T.idn[0:64, 0:64], True, True)], ("kb" + h, "idn"), ("bTp" + h,), ("pM" + h,))
+            V(64, TS(B("bT" + h), pM[:, 128:192], 1.0, T.m15[:], O.max, O.mult), ("bTp" + h, "m15"), ("bT" + h,), ("pM" + h,))
+            P(64, [MM(pU[:, 64:128], T.bm[:], B("bT" + h), True, True)], ("bT" + h, "bm"), ("bB" + h,), ("pU" + h,))
+            acc = B("acc" + h)
+            V(64, TT(acc, B("key" + h), pU[:, 64:128], O.is_equal), ("key" + h, "bB" + h), ("acc" + h,), ("pU" + h,))
+            P(128, [MM(p37[:, 384:448], T.bm[:], acc, True, True), MM(p37[:, 448:512], T.ones[:], acc, True, True)],
+              ("acc" + h, "bm", "ones"), ("okB" + h,), ("p37" + h,))
+            AP = T["AP" + h]
+            for k in range(1, 7):
+                V(64, TT(AP[:, 64 * k:64 * k + 64], acc, pV[:, 64 * k - 64:64 * k], O.mult), ("acc" + h, "P%d%s" % (k, h)), ("AP%d%s" % (k, h),), ("pV" + h,))
+            S(64, ACT(B("okS" + h), p37[:, 384:448], AF.Copy), ("okB" + h,), ("okS" + h,), ("p37" + h,))
+            S(64, ACT(B("nok" + h), p37[:, 384:448], AF.Copy, scale=-1.0, bias=1.0), ("okB" + h,), ("nok" + h,), ("p37" + h,))
+            if not last:
+                V(64, lambda a_=B("asum" + h), b_=p37[:, 448:512]: g.vector.tensor_reduce(a_, b_, AxisListType.X, O.add), ("okB" + h,), ("asum" + h,), ("p37" + h,))
+            apt = tuple("AP%d%s" % (k, h) for k in range(7))
+            P(320, [MM(pU[:, 192:512], T.bm[:], AP[:, 64:384], True, True)], apt[1:6] + ("bm",), ("Pst" + h,), ("pU" + h,))
+            P(768, [MM(p37[:, 0:384], T.bm[:], AP[:, 64:448], True, False), MM(p37[:, 0:384], T.nbm[:], AP[:, 0:384], False, True)],
+              apt + ("bm", "nbm"), ("Nst" + h,), ("p37" + h,))
+            V(64, TT(B("aL" + h), acc, pV[:, 384:448], O.mult), ("acc" + h, "L" + h), ("aL" + h,), ("pV" + h,))
+            if EQS[h]:
+                for k in range(1, 6):
+                    S(64, ACT(T["SQ" + h][:, 64 * k - 64:64 * k], pU[:, 128 + 64 * k:192 + 64 * k], AF.Square, bias=T.nq[:, k:k + 1]),
+                      ("Pst" + h, "nq"), ("SQ%d%s" % (k, h),), ("pU" + h,))
+                S(320, ACT(T["EQ" + h][:, 64:384], T["SQ" + h][:], AF.Relu, scale=-1.0, bias=T.onec[:]), tuple("SQ%d%s" % (k, h) for k in range(1, 6)) + ("onec",),
+                  tuple("EQ%d%s" % (k, h) for k in range(1, 6)))
+            else:
+                for k in range(1, 6):
+                    V(64, TS(T["EQ" + h][:, 64 * k:64 * k + 64], pU[:, 128 + 64 * k:192 + 64 * k], T.qk[:, k:k + 1], None, O.is_equal),
+                      ("Pst" + h, "qk%d" % k), ("EQ%d%s" % (k, h),), ("pU" + h,))
+            V(384, TT(T["EN" + h][:], T["EQ" + h][:], p37[:, 0:384], O.mult), ("Nst" + h,) + tuple("EQ%d%s" % (k, h) for k in range(6)), ("EN" + h,), ("p37" + h,))
+            V(64, TT(B("nokL" + h), B("nok" + h), pV[:, 384:448], O.mult), ("nok" + h, "L" + h), ("nokL" + h,), ("pV" + h,))
+            P(512, [MM(p37[:, 384:448], T.idn[:], B("nokL" + h), True, False), MM(p37[:, 384:448], T.bm[:], acc, False, False)]
+              + [MM(p37[:, 384:448], T.idn[:], T["EN" + h][:, 64 * k:64 * k + 64], False, k == 5) for k in range(6)],
+              ("EN" + h, "nokL" + h, "acc" + h, "idn", "bm"), ("ls" + h,), ("p37" + h,))
+            S(64, ACT(T[sL][:], p37[:, 384:448], AF.Copy), ("ls" + h,), (sL,), ("p37" + h,))
+            if not last:
+                send(sL, "in%dL%s" % (t + 1, h), "arr%dL%s" % (t + 1, h), 1, (sL,))
+            else:
+                dma("y", T.yl[:, o:o + H2], T[sL][:], (sL,), ())
+            P(256, [MM(pM[:, 64 * l:64 * l + 64], T.hsh[:, 128 * l:128 * l + 128], C, True, True) for l in range(4)], (ct, "hsh"), ("SH" + h,), ("pM" + h,))
+            P(64, [MM(pM[:, 320:384], T.tri[:], B("aL" + h), True, True)], ("aL" + h, "tri"), ("sh" + h,), ("pM" + h,))
+            for l in range(1, 5):
+                S(64, ACT(T["ES" + h][:, 64 * l - 64:64 * l], pM[:, 320:384], AF.Sign, bias=T.half[:, l:l + 1]), ("sh" + h, "half%d" % l), ("ES%d%s" % (l, h),), ("pM" + h,))
+            V(256, TT(T["EC" + h][:], T["ES" + h][:], pM[:, 0:256], O.mult), ("SH" + h,) + tuple("ES%d%s" % (l, h) for l in range(1, 5)), ("EC" + h,), ("pM" + h,))
+            P(384, [MM(pM[:, 384:448], T.hid[:, 0:128], C, True, False), MM(pM[:, 384:448], T.hid[:, 128:256], C, False, False)]
+              + [MM(pM[:, 384:448], T.idn[:], T["EC" + h][:, 64 * l:64 * l + 64], False, l == 3) for l in range(4)],
+              ("EC" + h, "idn", "hid0", "hid1", ct), ("cs" + h,), ("pM" + h,))
+            S(64, ACT(T[sC][:], pM[:, 384:448], AF.Copy), ("cs" + h,), (sC,), ("pM" + h,))
+            if not last:
+                send(sC, "in%dC%s" % (t + 1, h), "arr%dC%s" % (t + 1, h), 1, (sC,))
+            else:
+                dma("y", T.yc[:, o:o + H2], T[sC][:], (sC,), ())
+            S(64, ACT(B("aM" + h), acc, AF.Copy, scale=T.q6[:]), ("acc" + h, "q6"), ("aM" + h,))
+            P(1024, [MM(tb[:, 0:8], T.Em[:, 128 * a:128 * a + 128], B("aM" + h, a, 128, 16), a == 0, a == 15) for a in range(16)],
+              ("aM" + h, "acc" + h) + EM, ("tb" + h,), (tbn,))
+            V(4, TT(T["voff" + h][:], tb[:, 0:4], B("Kv" + h), O.add), ("tb" + h, "Kv" + h), ("voff" + h,), (tbn,))
+            V(4, CP(B("tt" + h), tb[:, 4:8]), ("tb" + h,), ("okd" + h,), (tbn,))
+            add("s", 0.16, [lambda o_=B("Vsel" + h), v_=T["VS" + h], f_=T["voff" + h]: g.scalar.activation(o_, v_[:, 0:6144].indirect(f_[:, 0:4]), AF.Copy)],
+                vt + ("voff" + h,), ("Vsel" + h,))
+            P(1024, [MM(tb[:, 8:12], T.Wm[:, 128 * a:128 * a + 128], B("Vsel" + h, a, 64, 16), a == 0, a == 15) for a in range(16)],
+              ("Vsel" + h,) + WM, ("hd" + h,), (tbn,))
+            V(4, CP(B("h0" + h), tb[:, 8:12]), ("hd" + h,), ("h0" + h,), (tbn,))
+            V(4, TS(B("h1" + h), B("h0" + h), 31, None, O.bitwise_and), ("h0" + h,), ("h1" + h,))
+            V(4, TT(B("h2" + h), B("h1" + h), B("K1" + h), O.add), ("h1" + h, "K1" + h), ("h2" + h,))
+            V(4, TT(B("h3" + h), B("h2" + h), B("tt" + h), O.mult), ("h2" + h, "okd" + h), ("h3" + h,))
+            V(4, TT(T["toff" + h][:], B("h3" + h), B("K2" + h), O.add), ("h3" + h, "K2" + h), ("toff" + h,))
+            if not last:
+                add("v", 0.25, [lambda f_=T["toff" + h], i_=B("Vsel" + h): g.vector.tensor_copy(T.X[:, 0:4224].indirect(f_[:, 0:4]), i_)],
+                    ("toff" + h, "Vsel" + h, "Xd"), ("X",))
+            else:
+                add("s", 0.16, [lambda o_=B("xo" + h), f_=T["toff" + h]: g.scalar.activation(o_, T.X[:, 0:4224].indirect(f_[:, 0:4]), AF.Copy)],
+                    ("X", "Xd", "toff" + h), ("xo" + h,))
+                V(128, TT(B("xd" + h), B("Vsel" + h), B("xo" + h), O.subtract), ("Vsel" + h, "xo" + h), ("xd" + h,))
+                V(128, TT(B("xe" + h), B("xd" + h), B("okS" + h), O.mult), ("xd" + h, "okS" + h), ("xe" + h,))
+                V(128, TT(B("yss" + h), B("xe" + h), B("S0" + h), O.add), ("xe" + h, "S0" + h), ("yss" + h,))
+                dma("s", T.ys[:, o:o + H2], B("yss" + h), ("yss" + h,), ())
+            Fp = pV[:, 448:512]
+            V(64, TT(B("fd" + h), B("Vsel" + h), Fp, O.subtract), ("Vsel" + h, "F" + h), ("fd" + h,), ("pV" + h,))
+            V(128, TT(B("xd" + h), B("fd" + h), B("okS" + h), O.mult), ("fd" + h, "okS" + h), ("xd" + h,))
+            V(64, TS(B("fi" + h), B("xd" + h), 0.5, -0.25, O.mult, O.add), ("xd" + h,), ("fi" + h,))
+            if not last:
+                V(64, TT(B("Fs" + h), B("fi" + h), Fp, O.add), ("fi" + h, "F" + h), ("Fs" + h,), ("pV" + h,))
+                V(64, TT(Fp, B("fi" + h), Fp, O.add), ("fi" + h, "F" + h), ("F" + h,), ("pV" + h,))
+            else:
+                V(64, TT(B("yfs" + h), B("fi" + h), Fp, O.add), ("fi" + h, "F" + h), ("yfs" + h,), ("pV" + h,))
+                dma("s", T.yf[:, o:o + H2], B("yfs" + h), ("yfs" + h,), ())
+
+    n = len(ops)
+    succ = [[] for _ in range(n)]
+    for k, p in enumerate(ops):
+        for d in p["all"]:
+            succ[d].append(k)
+    prio = [0.0] * n
+    for k in range(n - 1, -1, -1):
+        prio[k] = ops[k]["cost"] + 0.08 + max([prio[s] for s in succ[k]], default=0.0)
+    left = [len(p["all"]) for p in ops]
+    ready = [0.0] * n
+    free, pool, order = {}, {}, []
+    for k in range(n):
+        if left[k] == 0:
+            pool.setdefault(ops[k]["q"], []).append(k)
+    while len(order) < n:
+        best = None
+        for q, lst in pool.items():
+            if lst:
+                s0 = max(free.get(q, 0.0) if q != "r" else 0.0, min(ready[k] for k in lst))
+                if best is None or s0 < best[0]:
+                    best = (s0, q)
+        s0, q = best
+        k = max((k for k in pool[q] if ready[k] <= s0 + 0.02), key=lambda k: prio[k])
+        s0 = max(s0, ready[k])
+        pool[q].remove(k)
+        order.append(k)
+        hold = 0.1 if (ops[k]["sem"] is not None and q != "r") else ops[k]["cost"]
+        free[q] = s0 + hold
+        end = s0 + ops[k]["cost"]
+        for s in succ[k]:
+            ready[s] = max(ready[s], end + (0.06 if ops[s]["q"] == q else 0.12))
+            left[s] -= 1
+            if left[s] == 0:
+                pool.setdefault(ops[s]["q"], []).append(s)
+    count = {q: 0 for q in qsem}
+    know = {q: {} for q in eng}
+    done, seen = {}, {}
+    for k in order:
+        p = ops[k]
+        q = p["q"]
+        if q == "r":
+            done[k], seen[k] = p["sem"], {}
+            continue
+        need, via = {}, {}
+        for d in p["deps"]:
+            if done[d] is None:
+                continue
+            s, v = done[d]
+            if know[q].get(s, 0) < v:
+                need[s] = max(need.get(s, 0), v)
+                for s2, v2 in seen[d].items():
+                    via[s2] = max(via.get(s2, 0), v2)
+        for s, v in need.items():
+            eng[q].wait_ge(T.sem[s], v)
+            know[q][s] = max(know[q].get(s, 0), v)
+        for s, v in via.items():
+            know[q][s] = max(know[q].get(s, 0), v)
+        seen[k] = dict(know[q])
+        if p["sem"] is not None:
+            s, v = p["sem"]
+            ins = p["fns"][0]()
+            if v is None:
+                done[k] = None
+            else:
+                ins.then_inc(T.sem[s], v)
+                done[k] = (s, v)
+        else:
+            for f in p["fns"]:
+                f().then_inc(T.sem[qsem[q]], 1)
+                count[q] += 1
+            done[k] = (qsem[q], count[q])
+    for q, s in qsem.items():
+        g.wait_ge(T.sem[s], count[q])
+    for j in range(ndma[0]):
+        g.wait_ge(T.sem["d%d" % j], 16)
+    for p in ops:
+        if p["q"] == "r":
+            g.wait_ge(T.sem[p["sem"][0]], p["sem"][1])
+    g.wait_ge(T.sem.loc, loc[0])

@@ -2,9 +2,9 @@ import numpy as np
 from concourse.mybir import dt, AluOpType as O, AxisListType, ActivationFunctionType as AF
 
 H2 = 64
-NV = {"A": 4, "B": 10}
+NV = {"A": 4, "B": 8}
 EQS = {"A": 1, "B": 0}
-LV = {"A": (1,), "B": (1, 2)}
+LV = {"A": (1, 2), "B": (1, 2)}
 TILE = (1, 1, 2, 3, 3, 3)
 WID = {1: 10, 2: 12, 3: 15}
 RR = {1: list(range(8, -1, -1)), 2: list(range(12, 2, -1)) + [17], 3: list(range(16, 3, -1)) + [18]}
@@ -13,17 +13,17 @@ SEMAPHORES = ["sv", "ss", "st_", "sg", "loc", "arst1", "arst2"] + ["arr%d%s%s" %
 SEMAPHORES += ["d%d" % k for k in range(16)]
 _BF, _F32, _I32 = "bfloat16", "float32", "int32"
 for _n, _c, _d in (("X", 4096 + 128, _BF), ("chs", 128, _BF), ("sps", 128, _BF), ("fls", 128, _BF), ("wts", 1, _BF), ("stI", 128, _I32),
-                   ("st16", 128, "uint16"), ("stin1", 128, "uint16"), ("stin2", 128, "uint16"), ("pI", 1, _I32), ("aI", 1, _I32),
-                   ("qc", 1, _F32), ("qk", 6, _F32), ("nq", 6, _F32), ("iz", 1, _F32), ("q6", 1, _F32), ("q16", 1, _F32), ("m15", 1, _F32),
+                   ("st16", 128, "uint16"), ("stin1", 128, "uint16"), ("stin2", 128, "uint16"), ("pI", 1, _I32), ("aI", 1, _I32), ("jneg", 6, _F32),
+                   ("qc", 1, _F32), ("qk", 6, _F32), ("nq", 6, _F32), ("iz", 1, _F32), ("q6", 1, _F32), ("q16", 1, _F32),
                    ("ones", 128, _BF), ("bm0", 128, _BF), ("bm", 128, _BF), ("nbm", 128, _BF), ("idn", 128, _BF), ("nid", 128, _BF),
                    ("tri", 128, _BF), ("shm", 512, _BF), ("hsd", 512, _BF), ("hsh", 512, _BF), ("hid", 256, _BF), ("kc", 128, _BF),
-                   ("thr", 4, _F32), ("half", 5, _F32), ("onec", 1, _F32), ("g8", 8, _F32), ("g8w", 8, _F32), ("Wm", 2048, _BF), ("Em", 2048, _BF),
+                   ("half", 5, _F32), ("onec", 1, _F32), ("g8", 8, _F32), ("g8w", 8, _F32), ("Wm", 2048, _BF), ("Em", 2048, _BF), ("Es", 2048, _BF),
                    ("jrow", 18, _F32), ("cqx", 18, _F32), ("dif", 17, _F32), ("dif8", 19, _F32), ("Rm", 19 * 128, _BF), ("il0", 4, _F32),
-                   ("il", 4, _F32), ("m6", 1536, _BF), ("m16", 128, _BF)):
+                   ("il", 4, _F32), ("m6", 1536, _BF), ("m16", 64, _BF)):
     SCRATCH[_n] = ("sbuf", [128, _c], _d)
 _PACK = {}
-_SMALL = {_BF: (("w", 64), ("b", 64), ("key", 64), ("fk", 64), ("Kp", 64), ("bT", 64), ("okS", 64), ("aL", 64), ("aM", 64), ("acc", 64),
-                ("nok", 64), ("nokL", 64), ("Vsel", 64), ("xo", 64), ("yfs", 64), ("Fs", 64), ("kb", 128)),
+_SMALL = {_BF: (("w", 64), ("b", 64), ("key", 64), ("Kp", 64), ("okS", 64), ("aL", 64), ("aM", 64), ("acc", 64), ("nok", 64), ("nokL", 64),
+                ("Vsel", 64), ("xo", 64), ("yfs", 64), ("Fs", 64), ("kb", 64), ("kt", 64), ("aT", 64), ("kq", 128)),
           _F32: (("stf", 64), ("sta", 64), ("tt", 4), ("fd", 64), ("asum", 1), ("K1", 4), ("K2", 4), ("Kv", 4), ("S0", 64), ("yss", 64),
                  ("base", 64), ("xd", 64), ("xe", 64), ("t1", 64)),
           _I32: (("n1", 64), ("k8", 64), ("h0", 4), ("h1", 4), ("h2", 4), ("h3", 4), ("fi", 64), ("s0", 64), ("s1", 64), ("t2", 64), ("t4", 64), ("t5", 64))}
@@ -117,6 +117,9 @@ def rank_program(g, core, T, topo):
     def SCAN(out, d0, d1, o0, o1):
         return lambda: g.vector.tensor_tensor_scan(out, d0, d1, 0.0, o0, o1)
 
+    def TURN(out, a):
+        return lambda: g.vector.transpose(out, a)
+
     def ACT(out, in_, f, **kw):
         return lambda: g.scalar.activation(out, in_, f, **kw)
 
@@ -131,6 +134,9 @@ def rank_program(g, core, T, topo):
     def aff(out, in_, pat, cmp, base, cm, r, w):
         return add("g", 0.4, [lambda: g.affine_select(out, in_, pat, cmp, 0.0, base, cm)], r, w)
 
+    def iota(out, pat, base, cost, w):
+        add("g", cost, [lambda: g.iota(out, pat, base, 0, allow_small_or_imprecise_dtypes=True)], (), w)
+
     NE = min(len(topo.engines(core, c)) for c in T.cores if c != core)
 
     def send(name_in, name_out, sem, hop, r):
@@ -139,7 +145,7 @@ def rank_program(g, core, T, topo):
         lanes = sum(1 << e for e in topo.engines(core, dst)[:NE])
         loc[0] += NE
         k = add("g", 0.3, [lambda: g.remote_dma(T[name_out][:], T[name_in][:], T.sem[sem], T.sem.loc, pid, rid, lanes)], r, (), sem=("loc", None))
-        return add("r", 2.5, [], (), (name_out,), sem=(sem, NE), extra=(k,))
+        return add("r", 3.5, [], (), (name_out,), sem=(sem, NE), extra=(k,))
 
     dma("s", T.stI[:], T.st[:], (), ("stI",))
     dma("y", T.sps[:], T.sp[:], (), ("sps",))
@@ -152,18 +158,16 @@ def rank_program(g, core, T, topo):
     send("st16", "stin1", "arst1", 1, ("st16",))
     send("st16", "stin2", "arst2", 2, ("st16",))
     add("g", 0.2, [lambda: g.iota(T.pI[:], [[0, 1]], 0, 1)], (), ("pI",))
-    add("g", 0.2, [lambda: g.iota(T.jrow[:], [[1, 18]], -1, 0, allow_small_or_imprecise_dtypes=True)], (), ("jrow",))
-    add("g", 0.2, [lambda: g.iota(T.il0[:], [[16, 4]], 0, 0, allow_small_or_imprecise_dtypes=True)], (), ("il0",))
+    iota(T.jrow[:], [[1, 18]], -1, 0.2, ("jrow",))
+    iota(T.jneg[:], [[-1, 6]], 0, 0.2, ("jneg",))
+    iota(T.il0[:], [[16, 4]], 0, 0.2, ("il0",))
     V(64, MS(T.ones[:], 1.0), (), ("ones",))
     V(1, TS(T.aI[:], T.pI[:], 15, None, O.bitwise_and), ("pI",), ("aI",))
     V(1, CP(T.qc[:], T.aI[:]), ("aI",), ("qc",))
-    for k in range(6):
-        V(1, TS(T.qk[:, k:k + 1], T.qc[:], float(-k), None, O.add), ("qc",), ("qk%d" % k,))
+    V(6, TS(T.qk[:], T.jneg[:], T.qc[:], None, O.add), ("jneg", "qc"), tuple("qk%d" % k for k in range(6)))
+    V(5, TS(T.half[:], T.jneg[:, 0:5], 0.5, None, O.add), ("jneg",), tuple("half%d" % l for l in range(5)))
     V(1, MS(T.onec[:], 1.0), (), ("onec",))
-    for l in range(5):
-        V(1, MS(T.half[:, l:l + 1], 0.5 - l), (), ("half%d" % l,))
     V(1, TS(T.iz[:], T.qc[:], 0.0, None, O.is_equal), ("qc",), ("iz",))
-    V(1, TS(T.m15[:], T.qc[:], 15.0, None, O.is_equal), ("qc",), ("m15",))
     V(1, TS(T.q6[:], T.qc[:], 6.0, None, O.mult), ("qc",), ("q6",))
     V(1, TS(T.q16[:], T.qc[:], -1.0, 16.0, O.mult, O.add), ("qc",), ("q16",))
     V(6, TS(T.nq[:], T.qk[:], -1.0, None, O.mult), tuple("qk%d" % k for k in range(6)), ("nq",))
@@ -193,6 +197,7 @@ def rank_program(g, core, T, topo):
         S(16, ACT(T.Em[:, sl], T.ones[:, 0:16], AF.Copy, scale=T.g8[:, gg:gg + 1]), ("g8", "Ez", "ones"), ("Em%d" % gg,))
     EM = tuple("Em%d" % m for m in range(8))
     WM = tuple("Wm%d" % m for m in range(8))
+    V(1024, TS(T.Es[:], T.Em[:], 160.0, None, O.mult), EM, ("Es",))
     V(64, MS(T.kc[0:64, :], -512.0), (), ("kc0",))
     V(64, MS(T.kc[64:128, :], 0.0625), (), ("kc1",))
     V(64, TS(T.nid[:], T.idn[:], -1.0, None, O.mult), ("idn",), ("nid",))
@@ -219,7 +224,7 @@ def rank_program(g, core, T, topo):
                 if q == 1:
                     V(n * 32, MS(T[x][:], 1.0), (), (x,))
                 else:
-                    add("g", 0.13 + n * 128 * CS, [lambda x_=T[x], n_=n: g.iota(x_[:], [[0, 64 * n_]], 1, 0, allow_small_or_imprecise_dtypes=True)], (), (x,))
+                    iota(T[x][:], [[0, 64 * n]], 1, 0.13 + n * 128 * CS, (x,))
             S(64, ACT(T[a][:, 0::n], T.ones[:, 0:64], AF.Copy, scale=64.0), ("ones",), (a,))
             S(64, ACT(T[b][:, 1::n], T.ones[:, 0:64], AF.Copy, scale=0.0), ("ones",), (b,))
             S(64, ACT(T[l][:, 0::n], T.ones[:, 0:64], AF.Copy, scale=0.0), ("ones",), (l + "z",))
@@ -231,8 +236,9 @@ def rank_program(g, core, T, topo):
         V(1, MS(B("asum" + h), 0.0), (), ("asum" + h,))
         V(64, CP(T["pV" + h][:, 448:512], T.fls[:, H2 * hi:H2 * hi + H2]), ("fls",), ("F" + h,), ("pV" + h,))
         V(64, CP(B("Fs" + h), T.fls[:, H2 * hi:H2 * hi + H2]), ("fls",), ("Fs" + h,))
-        V(64, TS(T.thr[:, hi:hi + 1], T.qc[:], NV[h] - 0.5, None, O.is_ge), ("qc",), ("thr0" + h,))
-        V(64, TS(T.thr[:, 2 + hi:3 + hi], T.thr[:, hi:hi + 1], -7.5, 8.5, O.mult, O.add), ("thr0" + h,), ("thr" + h,))
+        V(64, MS(B("kq" + h), -1.25), (), ("kq" + h,))
+        for m in range(NV[h]):
+            V(64, MS(B("kq" + h, m, 128, 16), -10.625), (), ("kq" + h,))
 
     def rec(t, h):
         o = H2 * "AB".index(h)
@@ -356,19 +362,17 @@ def rank_program(g, core, T, topo):
                 V(64, TT(T["ind" + h][:, 64 * m:64 * m + 64], vm(h, m), pV[:, 448:512], O.is_ge), vt + ("F" + h,), ("ind%d%s" % (m, h),), ("pV" + h,))
             prev = ()
             for c in range(2):
-                prev = (P(512, [MM(pU[:, 0:64], T.Em[:, 128 * m:128 * m + 128], T["ind" + h][:, 64 * m:64 * m + 64], m == 0, m == 15) for m in range(8 * c, 8 * c + 8)],
-                          tuple("ind%d%s" % (m, h) for m in range(8 * c, 8 * c + 8)) + EM, ("cnt%d%s" % (c, h),), ("pU" + h,), after=prev),)
-            V(64, TS(B("fk" + h), pU[:, 0:64], T.thr[:, 2 + hi:3 + hi], None, O.is_ge), ("cnt0" + h, "cnt1" + h, "thr" + h), ("fk" + h,), ("pU" + h,))
-            V(128, TT(B("key" + h), B("fk" + h), B("Kp" + h), O.mult), ("fk" + h, "Kp" + h), ("key" + h,))
-            big, kat, _ = _PACK["kb" + h]
-            kb = T[big][0:64, kat:kat + 128]
-            P(128, [MM(pM[0:64, 0:128], B("key" + h), T.idn[:], True, True)], ("key" + h, "idn"), ("kT" + h,), ("pM" + h,))
-            V(128, SCAN(kb, T.m16[0:64, :], pM[0:64, 0:128], O.mult, O.max), ("kT" + h, "m16"), ("kb" + h,), ("pM" + h,))
-            P(64, [MM(pM[:, 128:192], kb, T.idn[0:64, 0:64], True, True)], ("kb" + h, "idn"), ("bTp" + h,), ("pM" + h,))
-            V(64, TS(B("bT" + h), pM[:, 128:192], 1.0, T.m15[:], O.max, O.mult), ("bTp" + h, "m15"), ("bT" + h,), ("pM" + h,))
-            P(64, [MM(pU[:, 64:128], T.bm[:], B("bT" + h), True, True)], ("bT" + h, "bm"), ("bB" + h,), ("pU" + h,))
-            acc = B("acc" + h)
-            V(64, TT(acc, B("key" + h), pU[:, 64:128], O.is_equal), ("key" + h, "bB" + h), ("acc" + h,), ("pU" + h,))
+                prev = (P(512, ([MM(pU[:, 0:64], B("kq" + h), T.ones[:, 0:64], True, False)] if c == 0 else [])
+                          + [MM(pU[:, 0:64], T.Es[:, 128 * m:128 * m + 128], T["ind" + h][:, 64 * m:64 * m + 64], False, m == 15) for m in range(8 * c, 8 * c + 8)],
+                          tuple("ind%d%s" % (m, h) for m in range(8 * c, 8 * c + 8)) + ("Es", "kq" + h, "ones"), ("cnt%d%s" % (c, h),), ("pU" + h,), after=prev),)
+            V(64, TT(B("key" + h), pU[:, 0:64], B("Kp" + h), O.min), ("cnt0" + h, "cnt1" + h, "Kp" + h), ("key" + h,), ("pU" + h,))
+            kb, acc = B("kb" + h), B("acc" + h)
+            V(64, TURN(B("kt" + h), B("key" + h)), ("key" + h,), ("kt" + h,))
+            V(64, SCAN(kb, T.m16[:], B("kt" + h), O.mult, O.max), ("kt" + h, "m16"), ("kb" + h,))
+            for j in range(4):
+                V(64, TS(B("aT" + h, 16 * j, 16 * j + 16), B("kt" + h, 16 * j, 16 * j + 16), B("kb" + h, 16 * j + 15, 16 * j + 16), None, O.is_equal),
+                  ("kt" + h, "kb" + h), ("aT%d%s" % (j, h),))
+            V(64, TURN(acc, B("aT" + h)), tuple("aT%d%s" % (j, h) for j in range(4)), ("acc" + h,))
             P(128, [MM(p37[:, 384:448], T.bm[:], acc, True, True), MM(p37[:, 448:512], T.ones[:], acc, True, True)],
               ("acc" + h, "bm", "ones"), ("okB" + h,), ("p37" + h,))
             AP = T["AP" + h]
@@ -458,7 +462,7 @@ def rank_program(g, core, T, topo):
             succ[d].append(k)
     prio = [0.0] * n
     for k in range(n - 1, -1, -1):
-        prio[k] = ops[k]["cost"] + 0.08 + max([prio[s] for s in succ[k]], default=0.0)
+        prio[k] = ops[k]["cost"] + 0.1 + max([prio[s] for s in succ[k]], default=0.0)
     left = [len(p["all"]) for p in ops]
     ready = [0.0] * n
     free, pool, order = {}, {}, []
@@ -481,7 +485,7 @@ def rank_program(g, core, T, topo):
         free[q] = s0 + hold
         end = s0 + ops[k]["cost"]
         for s in succ[k]:
-            ready[s] = max(ready[s], end + (0.06 if ops[s]["q"] == q else 0.12))
+            ready[s] = max(ready[s], end + (0.15 if ops[s]["q"] == q else 0.25))
             left[s] -= 1
             if left[s] == 0:
                 pool.setdefault(ops[s]["q"], []).append(s)

import numpy as np
from concourse.mybir import dt, AluOpType as O, AxisListType, ActivationFunctionType as AF

H2 = 64
NV = {"A": 4, "B": 8}
EQS = {"A": 1, "B": 0}
LV = {"A": (1, 2), "B": (1, 2)}
TILE = (1, 1, 2, 3, 3, 3)
WID = {1: 10, 2: 12, 3: 15}
RR = {1: list(range(8, -1, -1)), 2: list(range(12, 2, -1)) + [17], 3: list(range(16, 3, -1)) + [18]}
SCRATCH = {}
SEMAPHORES = ["sv", "ss", "st_", "sg", "loc", "arst1", "arst2"] + ["arr%d%s%s" % (t, x, h) for t in (1, 2) for x in "LC" for h in "AB"]
SEMAPHORES += ["d%d" % k for k in range(16)]
_BF, _F32, _I32 = "bfloat16", "float32", "int32"
for _n, _c, _d in (("X", 4096 + 128, _BF), ("chs", 128, _BF), ("sps", 128, _BF), ("fls", 128, _BF), ("wts", 1, _BF), ("stI", 128, _I32),
                   ("st16", 128, "uint16"), ("stin1", 128, "uint16"), ("stin2", 128, "uint16"), ("pI", 1, _I32), ("aI", 1, _I32), ("jneg", 6, _F32),
                   ("qc", 1, _F32), ("qk", 6, _F32), ("nq", 6, _F32), ("iz", 1, _F32), ("q6", 1, _F32), ("q16", 1, _F32),
                   ("ones", 128, _BF), ("bm0", 128, _BF), ("bm", 128, _BF), ("nbm", 128, _BF), ("idn", 128, _BF), ("nid", 128, _BF),
                   ("tri", 128, _BF), ("shm", 512, _BF), ("hsd", 512, _BF), ("hsh", 512, _BF), ("hid", 256, _BF), ("kc", 128, _BF),
                   ("half", 5, _F32), ("onec", 1, _F32), ("g8", 8, _F32), ("g8w", 8, _F32), ("Wm", 2048, _BF), ("Em", 2048, _BF), ("Es", 2048, _BF),
                   ("jrow", 18, _F32), ("cqx", 18, _F32), ("dif", 17, _F32), ("dif8", 19, _F32), ("Rm", 19 * 128, _BF), ("il0", 4, _F32),
                   ("il", 4, _F32), ("m6", 1536, _BF), ("m16", 64, _BF)):
    SCRATCH[_n] = ("sbuf", [128, _c], _d)
_PACK = {}
_SMALL = {_BF: (("w", 64), ("b", 64), ("key", 64), ("Kp", 64), ("okS", 64), ("aL", 64), ("aM", 64), ("acc", 64), ("nok", 64), ("nokL", 64),
                ("Vsel", 64), ("xo", 64), ("yfs", 64), ("Fs", 64), ("kb", 64), ("kt", 64), ("aT", 64), ("kq", 128)),
          _F32: (("stf", 64), ("sta", 64), ("tt", 4), ("fd", 64), ("asum", 1), ("K1", 4), ("K2", 4), ("Kv", 4), ("S0", 64), ("yss", 64),
                 ("base", 64), ("xd", 64), ("xe", 64), ("t1", 64)),
          _I32: (("n1", 64), ("k8", 64), ("h0", 4), ("h1", 4), ("h2", 4), ("h3", 4), ("fi", 64), ("s0", 64), ("s1", 64), ("t2", 64), ("t4", 64), ("t5", 64))}
for _h in "AB":
    for _d, _names in _SMALL.items():
        _at = 0
        for _n, _c in _names:
            _PACK[_n + _h] = ("pk" + _d[0] + _h, _at, _c)
            _at += -(-_c // 32) * 32
        SCRATCH["pk" + _d[0] + _h] = ("sbuf", [128, _at], _d)
    for _n, _c, _d in (("z", 6144, _BF), ("VS", 6144, _BF), ("ind", 1024, _BF), ("off", 64, "uint16"), ("mk", 960, _BF), ("co", 960, _BF),
                       ("AP", 448, _BF), ("ES", 256, _BF), ("EC", 256, _BF), ("EQ", 384, _BF), ("EN", 384, _BF), ("SQ", 320, _BF),
                       ("voff", 4, "uint16"), ("toff", 4, "uint16")):
        SCRATCH[_n + _h] = ("sbuf", [128, _c], _d)
    for _q in (1, 2, 3):
        for _n in ("L", "da", "db"):
            SCRATCH["%s%d%s" % (_n, _q, _h)] = ("sbuf", [128, 64 * WID[_q]], _BF)
    for _x in "LC":
        for _t in (0, 1, 2):
            SCRATCH["s%d%s%s" % (_t, _x, _h)] = ("sbuf", [128, 64], _BF)
        for _t in (1, 2):
            SCRATCH["in%d%s%s" % (_t, _x, _h)] = ("sbuf", [128, 64], _BF)
    for _n in ("pU", "p37", "pV", "pM"):
        SCRATCH[_n + _h] = ("psum", [128, 512], _F32)


def rank_program(g, core, T, topo):
    rank = T.rank_of(core)
    if rank is None:
        return
    N = len(T.cores)
    eng = {"v": g.vector, "s": g.scalar, "t": g.tensor, "y": g.sync, "g": g}
    qsem = {"v": "sv", "s": "ss", "t": "st_", "g": "sg"}
    CV, CS, CT = 0.00083 * 1.2, 0.00083 * 1.2, 0.00083 * 0.85
    GATH = 0.07 + 1024 * 1.56 * CS
    ops = []
    lastw, readers, bank = {}, {}, {}
    ndma, loc = [0], [0]

    def B(name, a=0, b=None, step=1):
        big, at, c = _PACK[name] if name in _PACK else (name, 0, SCRATCH[name][1][1])
        e = c if b is None else b
        return T[big][:, at + a:at + e:step] if step != 1 else T[big][:, at + a:at + e]

    def add(q, cost, fns, r=(), w=(), banks=(), sem=None, extra=(), after=()):
        k = len(ops)
        deps = set(extra)
        for x in r:
            if x in lastw:
                deps.add(lastw[x])
            readers.setdefault(x, []).append(k)
        for x in w:
            if x in lastw:
                deps.add(lastw[x])
            deps.update(readers.get(x, ()))
            lastw[x] = k
            readers[x] = []
        for x in banks:
            st = bank.setdefault(x, [None, [], []])
            if st[0] != q:
                st[0], st[1], st[2] = q, st[2], []
            deps.update(st[1])
            st[2].append(k)
        deps.discard(k)
        ops.append({"q": q, "cost": cost, "fns": fns, "deps": deps, "all": deps | set(after), "sem": sem})
        return k

    def V(n, fn, r, w, banks=(), **kw):
        return add("v", max(64, n) * CV, [fn], r, w, banks, **kw)

    def S(n, fn, r, w, banks=()):
        return add("s", 0.03 + max(40, n) * CS, [fn], r, w, banks)

    def P(cols, fns, r, w, banks=(), **kw):
        return add("t", 0.02 + cols * CT, fns, r, w, banks, **kw)

    def TS(out, in0, s1, s2, o0, o1=None):
        if o1 is None:
            return lambda: g.vector.tensor_scalar(out, in0, s1, None, o0)
        return lambda: g.vector.tensor_scalar(out, in0, s1, s2, o0, o1)

    def TT(out, a, b, op):
        return lambda: g.vector.tensor_tensor(out, a, b, op)

    def CP(out, a):
        return lambda: g.vector.tensor_copy(out, a)

    def MS(ap, c):
        return lambda: g.vector.memset(ap, c)

    def SCAN(out, d0, d1, o0, o1):
        return lambda: g.vector.tensor_tensor_scan(out, d0, d1, 0.0, o0, o1)

    def TURN(out, a):
        return lambda: g.vector.transpose(out, a)

    def ACT(out, in_, f, **kw):
        return lambda: g.scalar.activation(out, in_, f, **kw)

    def MM(out, l, r, a, z):
        return lambda: g.tensor.matmul(out, l, r, a, z)

    def dma(q, out, in_, r, w, cost=2.2):
        s = "d%d" % ndma[0]
        ndma[0] += 1
        return add(q, cost, [lambda: eng[q].dma_start(out, in_)], r, w, sem=(s, 16))

    def aff(out, in_, pat, cmp, base, cm, r, w):
        return add("g", 0.4, [lambda: g.affine_select(out, in_, pat, cmp, 0.0, base, cm)], r, w)

    def iota(out, pat, base, cost, w):
        add("g", cost, [lambda: g.iota(out, pat, base, 0, allow_small_or_imprecise_dtypes=True)], (), w)

    NE = min(len(topo.engines(core, c)) for c in T.cores if c != core)

    def send(name_in, name_out, sem, hop, r):
        dst = T.cores[(rank + hop) % N]
        rid, pid = topo.addr(dst)[:2]
        lanes = sum(1 << e for e in topo.engines(core, dst)[:NE])
        loc[0] += NE
        k = add("g", 0.3, [lambda: g.remote_dma(T[name_out][:], T[name_in][:], T.sem[sem], T.sem.loc, pid, rid, lanes)], r, (), sem=("loc", None))
        return add("r", 3.5, [], (), (name_out,), sem=(sem, NE), extra=(k,))

    dma("s", T.stI[:], T.st[:], (), ("stI",))
    dma("y", T.sps[:], T.sp[:], (), ("sps",))
    dma("y", T.X[:, 0:4096], T.x[:], (), ("X",), 6.0)
    dma("s", T.wts[:], T.wt[:], (), ("wts",))
    dma("s", T.chs[:], T.ch[:], (), ("chs",))
    dma("s", T.fls[:], T.fl[:], (), ("fls",))
    V(64, MS(T.X[:, 4096:4224], 0.0), (), ("Xd",))
    V(128, CP(T.st16[:], T.stI[:]), ("stI",), ("st16",))
    send("st16", "stin1", "arst1", 1, ("st16",))
    send("st16", "stin2", "arst2", 2, ("st16",))
    add("g", 0.2, [lambda: g.iota(T.pI[:], [[0, 1]], 0, 1)], (), ("pI",))
    iota(T.jrow[:], [[1, 18]], -1, 0.2, ("jrow",))
    iota(T.jneg[:], [[-1, 6]], 0, 0.2, ("jneg",))
    iota(T.il0[:], [[16, 4]], 0, 0.2, ("il0",))
    V(64, MS(T.ones[:], 1.0), (), ("ones",))
    V(1, TS(T.aI[:], T.pI[:], 15, None, O.bitwise_and), ("pI",), ("aI",))
    V(1, CP(T.qc[:], T.aI[:]), ("aI",), ("qc",))
    V(6, TS(T.qk[:], T.jneg[:], T.qc[:], None, O.add), ("jneg", "qc"), tuple("qk%d" % k for k in range(6)))
    V(5, TS(T.half[:], T.jneg[:, 0:5], 0.5, None, O.add), ("jneg",), tuple("half%d" % l for l in range(5)))
    V(1, MS(T.onec[:], 1.0), (), ("onec",))
    V(1, TS(T.iz[:], T.qc[:], 0.0, None, O.is_equal), ("qc",), ("iz",))
    V(1, TS(T.q6[:], T.qc[:], 6.0, None, O.mult), ("qc",), ("q6",))
    V(1, TS(T.q16[:], T.qc[:], -1.0, 16.0, O.mult, O.add), ("qc",), ("q16",))
    V(6, TS(T.nq[:], T.qk[:], -1.0, None, O.mult), tuple("qk%d" % k for k in range(6)), ("nq",))
    aff(T.bm0[:], T.ones[:], [[-16, 8], [0, 16]], O.is_ge, 0, 1, ("ones",), ("bm0",))
    aff(T.bm[:], T.bm0[:], [[16, 8], [0, 16]], O.is_ge, 15, -1, ("bm0",), ("bm",))
    aff(T.idn[:], T.ones[:], [[-1, 128]], O.is_equal, 0, 1, ("ones",), ("idn",))
    V(4, TS(T.il[:], T.il0[:], T.qc[:], None, O.add), ("il0", "qc"), ("il",))
    V(18, TS(T.cqx[:], T.jrow[:], T.qc[:], None, O.is_equal), ("jrow", "qc"), ("cqx",))
    V(17, TT(T.dif[:], T.cqx[:, 1:18], T.cqx[:, 0:17], O.subtract), ("cqx",), ("dif",))
    V(17, TS(T.dif8[:, 0:17], T.dif[:], 8.0, None, O.mult), ("dif",), ("dif8a",))
    V(2, TS(T.dif8[:, 17:19], T.cqx[:, 3:5], 8.0, None, O.mult), ("cqx",), ("dif8b",))
    for r in list(range(8, -1, -1)) + [17, 18] + list(range(16, 8, -1)):
        tok = ("bm", "dif8b" if r > 16 else "dif8a")
        if r < 9:
            V(64, TS(T.Rm[:, r * 128:(r + 1) * 128], T.bm[:], T.dif8[:, r:r + 1], None, O.mult), tok, ("Rm%d" % r,))
        else:
            S(128, ACT(T.Rm[:, r * 128:(r + 1) * 128], T.bm[:], AF.Copy, scale=T.dif8[:, r:r + 1]), tok, ("Rm%d" % r,))
    V(8, CP(T.g8[:], T.bm[:, 0::16]), ("bm",), ("g8",))
    V(8, TS(T.g8w[:], T.g8[:], T.wts[:], None, O.mult), ("g8", "wts"), ("g8w",))
    V(1024, MS(T.Wm[:], 0.0), (), ("Wz",))
    V(1024, MS(T.Em[:], 0.0), (), ("Ez",))
    for gg in range(8):
        sl = slice(16 * gg, 16 * gg + 15 * 129 + 1, 129)
        S(16, ACT(T.Wm[:, sl], T.ones[:, 0:16], AF.Copy, scale=T.g8w[:, gg:gg + 1]), ("g8w", "Wz", "ones"), ("Wm%d" % gg,))
    for gg in range(8):
        sl = slice(16 * gg, 16 * gg + 15 * 129 + 1, 129)
        S(16, ACT(T.Em[:, sl], T.ones[:, 0:16], AF.Copy, scale=T.g8[:, gg:gg + 1]), ("g8", "Ez", "ones"), ("Em%d" % gg,))
    EM = tuple("Em%d" % m for m in range(8))
    WM = tuple("Wm%d" % m for m in range(8))
    V(1024, TS(T.Es[:], T.Em[:], 160.0, None, O.mult), EM, ("Es",))
    V(64, MS(T.kc[0:64, :], -512.0), (), ("kc0",))
    V(64, MS(T.kc[64:128, :], 0.0625), (), ("kc1",))
    V(64, TS(T.nid[:], T.idn[:], -1.0, None, O.mult), ("idn",), ("nid",))
    V(64, TS(T.nbm[:], T.bm[:], -1.0, None, O.mult), ("bm",), ("nbm",))
    aff(T.tri[:], T.bm[:], [[1, 128]], O.is_ge, 0, -1, ("bm",), ("tri",))
    for l in range(1, 5):
        aff(T.shm[:, (l - 1) * 128:l * 128], T.bm[:], [[-1, 128]], O.is_equal, -l, 1, ("bm",), ("shm%d" % l,))
    for l in range(1, 5):
        V(256, TT(T.hsd[:, (l - 1) * 128:l * 128], T.shm[:, (l - 1) * 128:l * 128],
                  T.idn[:] if l == 1 else T.shm[:, (l - 2) * 128:(l - 1) * 128], O.subtract),
          ("shm%d" % l, "idn" if l == 1 else "shm%d" % (l - 1)), ("hsd%d" % l,))
    V(256, TS(T.hsh[:], T.hsd[:], 0.5, None, O.mult), ("hsd1", "hsd2", "hsd3", "hsd4"), ("hsh",))
    V(64, TS(T.hid[:, 0:128], T.idn[:], 0.5, None, O.mult), ("idn",), ("hid0",))
    V(64, TS(T.hid[:, 128:256], T.shm[:, 384:512], 0.5, None, O.mult), ("shm4",), ("hid1",))
    V(768, MS(T.m6[:], 1.0), (), ("m6",))
    V(256, MS(T.m6[:, 0::6], 0.0), (), ("m6",))
    V(64, MS(T.m16[:], 1.0), (), ("m16",))
    V(8, MS(T.m16[:, 0::16], 0.0), (), ("m16",))
    for hi, h in enumerate("AB"):
        for q in (1, 2, 3):
            n = WID[q]
            a, b, l = ("%s%d%s" % (x, q, h) for x in ("da", "db", "L"))
            for x in (a, b):
                if q == 1:
                    V(n * 32, MS(T[x][:], 1.0), (), (x,))
                else:
                    iota(T[x][:], [[0, 64 * n]], 1, 0.13 + n * 128 * CS, (x,))
            S(64, ACT(T[a][:, 0::n], T.ones[:, 0:64], AF.Copy, scale=64.0), ("ones",), (a,))
            S(64, ACT(T[b][:, 1::n], T.ones[:, 0:64], AF.Copy, scale=0.0), ("ones",), (b,))
            S(64, ACT(T[l][:, 0::n], T.ones[:, 0:64], AF.Copy, scale=0.0), ("ones",), (l + "z",))
        V(4, TS(B("K1" + h), T.il[:], 31.0, float(31 * H2 * hi - 4096), O.mult, O.add), ("il",), ("K1" + h,))
        V(4, TS(B("K2" + h), T.il[:], float(4096 + H2 * hi), None, O.add), ("il",), ("K2" + h,))
        V(4, TS(B("Kv" + h), T.il[:], 96.0, 5.0, O.mult, O.add), ("il",), ("Kv" + h,))
        V(64, MS(T["AP" + h][:, 0:64], 0.0), (), ("AP0" + h,))
        V(64, TS(T["EQ" + h][:, 0:64], T.ones[:, 0:64], T.iz[:], None, O.mult), ("ones", "iz"), ("EQ0" + h,))
        V(1, MS(B("asum" + h), 0.0), (), ("asum" + h,))
        V(64, CP(T["pV" + h][:, 448:512], T.fls[:, H2 * hi:H2 * hi + H2]), ("fls",), ("F" + h,), ("pV" + h,))
        V(64, CP(B("Fs" + h), T.fls[:, H2 * hi:H2 * hi + H2]), ("fls",), ("Fs" + h,))
        V(64, MS(B("kq" + h), -1.25), (), ("kq" + h,))
        for m in range(NV[h]):
            V(64, MS(B("kq" + h, m, 128, 16), -10.625), (), ("kq" + h,))

    def rec(t, h):
        o = H2 * "AB".index(h)
        if t == 0:
            return T.chs[:, o:o + H2], T.sps[:, o:o + H2], "chs", "sps"
        c, l = "in%dC%s" % (t, h), "in%dL%s" % (t, h)
        return T[c][:], T[l][:], c, l

    def vm(h, m):
        return T["VS" + h][:, 6 * m + 5::96]

    def entry(k, h):
        q = TILE[k]
        n = WID[q]
        L = "L%d%s" % (q, h)
        V(n * 32, SCAN(T["mk" + h][:, 0:64 * n], T["da%d%s" % (q, h)][:], T["db%d%s" % (q, h)][:], O.add, O.min),
          ("da%d%s" % (q, h), "db%d%s" % (q, h)), ("mk" + h,))
        V(n * 32, SCAN(T["co" + h][:, 0:64 * n], T["mk" + h][:, 0:64 * n], T[L][:], O.mult, O.add),
          ("mk" + h, L + "z") + tuple("%s_%d" % (L, r) for r in RR[q]), ("co" + h,))
        if k < 5:
            V(64, TS(B("w" + h), T["co" + h][:, n - 1:64 * n:n], 0.25, 2.0, O.mult, O.add), ("co" + h,), ("w" + h,))

    for t in range(3):
        last = t == 2
        for hi, h in enumerate("AB"):
            C, L, ct, lt = rec(t, h)
            pV, pM, pU, p37 = T["pV" + h], T["pM" + h], T["pU" + h], T["p37" + h]
            o = H2 * hi
            src, stt = ((T.stI, "stI"), (T.stin1, "stin1"), (T.stin2, "stin2"))[t]
            V(64, CP(B("stf" + h), src[:, o:o + H2]), (stt,), ("stf" + h,))
            V(64, TS(B("sta" + h), B("stf" + h), B("asumA"), B("asumB"), O.add, O.add), ("stf" + h, "asumA", "asumB"), ("sta" + h,))
            V(64, TS(B("base" + h), L, 613.0, None, O.mult), (lt,), ("base" + h,))
            V(128, TT(B("s0" + h), B("base" + h), B("sta" + h), O.add), ("base" + h, "sta" + h), ("s0" + h,))
            V(64, TS(B("s1" + h), B("s0" + h), 4095, None, O.bitwise_and), ("s0" + h,), ("s1" + h,))
            V(64, CP(T["off" + h][:], B("s1" + h)), ("s1" + h,), ("off" + h,))
            V(64, CP(pV[:, 384:448], L), (lt,), ("L" + h,), ("pV" + h,))
            S(64, ACT(B("Kp" + h), L, AF.Identity, scale=16.0, bias=T.q16[:]), (lt, "q16"), ("Kp" + h,))
            S(64, ACT(T["da1" + h][:, 1::10], L, AF.Copy, scale=T.iz[:]), (lt, "iz"), ("da1" + h,))
            S(64, ACT(T["db1" + h][:, 0::10], T.ones[:, 0:64], AF.Copy, scale=-8.0), ("ones",), ("db1" + h,))
            P(512, [MM(pM[:, 64 * j:64 * j + 64], T.Rm[:, (8 - j) * 128:(9 - j) * 128], C, True, True) for j in range(8)],
              (ct,) + tuple("Rm%d" % (8 - j) for j in range(8)), ("dM" + h,), ("pM" + h,))
            P(192, [MM(pU[:, 64 * j:64 * j + 64], T.Rm[:, r * 128:(r + 1) * 128], C, True, True) for j, r in enumerate((0, 17, 18))],
              (ct, "Rm0", "Rm17", "Rm18"), ("dU" + h,), ("pU" + h,))
            P(512, [MM(p37[:, 64 * j:64 * j + 64], T.Rm[:, (16 - j) * 128:(17 - j) * 128], C, True, True) for j in range(8)],
              (ct,) + tuple("Rm%d" % (16 - j) for j in range(8)), ("d37" + h,), ("p37" + h,))
            at = {r: (pM, 8 - r, "dM" + h, "pM" + h) for r in range(1, 9)}
            at.update({r: (p37, 16 - r, "d37" + h, "p37" + h) for r in range(9, 17)})
            at.update({r: (pU, j, "dU" + h, "pU" + h) for j, r in enumerate((0, 17, 18))})
            for q in (1, 2, 3):
                n = WID[q]
                todo = list(enumerate(RR[q]))
                for j, r in (todo if q == 1 else todo[::-1]):
                    ps, jj, tk, bk = at[r]
                    out, in_ = T["L%d%s" % (q, h)][:, 1 + j::n], ps[:, 64 * jj:64 * jj + 64]
                    low = r in (0, 17, 18)
                    if q in LV[h]:
                        V(64, TS(out, in_, -4.0, None, O.add) if low else CP(out, in_), (tk,), ("L%d%s_%d" % (q, h, r),), (bk,))
                    else:
                        S(64, ACT(out, in_, AF.Copy, bias=-4.0) if low else ACT(out, in_, AF.Copy), (tk,), ("L%d%s_%d" % (q, h, r),), (bk,))
            entry(0, h)
        for k in range(6):
            for h in "AB":
                pV, pU = T["pV" + h], T["pU" + h]
                n = WID[TILE[k]]
                c8 = T["co" + h][:, n - 1:64 * n:n]
                zk, z = "z%d%s" % (k, h), T["z" + h]
                add("s", GATH, [lambda o_=z[:, k::6], f_=T["off" + h]: g.scalar.activation(o_, T.X[:, 0:4096].indirect(f_[:, 0:64]), AF.Copy)],
                    ("X", "off" + h), (zk,))
                P(17 * 64, [MM(pU[:, 0:64], T.kc[:], T.ones[:, 0:64], True, False)]
                  + [MM(pU[:, 0:64], T.Wm[:, 128 * m:128 * m + 128], z[:, 6 * m + k::96], False, m == 15) for m in range(16)],
                  (zk, "kc0", "kc1", "ones") + WM, ("u" + h,), ("pU" + h,))
                y4 = pU[:, 0:64]
                if k < 5:
                    V(64, TT(B("t1" + h), y4, B("w" + h), O.mult), ("u" + h, "w" + h), ("t1" + h,), ("pU" + h,))
                    V(64, TS(pU[:, 64:128], y4, 37.0, -148.0, O.mult, O.add), ("u" + h,), ("t3" + h,), ("pU" + h,))
                    V(64, TS(B("t2" + h), B("t1" + h), 0.125, -0.9375, O.mult, O.add), ("t1" + h,), ("t2" + h,))
                    V(64, TT(B("t4" + h), B("t2" + h), pU[:, 64:128], O.add), ("t2" + h, "t3" + h), ("t4" + h,), ("pU" + h,))
                    V(64, TS(B("t5" + h), B("t4" + h), 4095, None, O.bitwise_and), ("t4" + h,), ("t5" + h,))
                    V(64, CP(T["off" + h][:], B("t5" + h)), ("t5" + h,), ("off" + h,))
                V(64, TT(B("k8" + h), y4, c8, O.add), ("u" + h, "co" + h), ("k8" + h,), ("pU" + h,))
                V(64, TS(B("n1" + h), B("k8" + h), 3, 3, O.arith_shift_right, O.bitwise_and), ("k8" + h,), ("n1" + h,))
                Pk, pt = pV[:, 64 * k:64 * k + 64], "P%d%s" % (k + 1, h)
                if k == 0:
                    V(64, CP(Pk, B("n1" + h)), ("n1" + h,), (pt,), ("pV" + h,))
                else:
                    V(64, TT(Pk, B("n1" + h), pV[:, 64 * k - 64:64 * k], O.add), ("n1" + h, "P%d%s" % (k, h)), (pt,), ("pV" + h,))
                if k < 5:
                    q = TILE[k + 1]
                    n2, da, db = WID[q], "da%d%s" % (q, h), "db%d%s" % (q, h)
                    V(64, TS(T[db][:, 0::n2], Pk, float(k + 1 - RR[q][0]), None, O.add), (pt,), (db,), ("pV" + h,))
                    V(64, TS(B("b" + h), Pk, T.qk[:, k + 1:k + 2], None, O.is_ge), (pt, "qk%d" % (k + 1)), ("b" + h,), ("pV" + h,))
                    V(64, TT(T[da][:, 1::n2], B("b" + h), pV[:, 384:448], O.mult), ("b" + h, "L" + h), (da,), ("pV" + h,))
                    entry(k + 1, h)
        if last:
            for hi, h in enumerate("AB"):
                pM = T["pM" + h]
                P(2048, [MM(pM[:, 0:64], T.idn[:], T.X[:, 2048 * hi + j:2048 * hi + 2048:32], j == 0, j == 31) for j in range(32)],
                  ("X", "idn"), ("sums" + h,), ("pM" + h,))
                V(64, CP(B("S0" + h), pM[:, 0:64]), ("sums" + h,), ("S0" + h,), ("pM" + h,))
        for hi, h in enumerate("AB"):
            C, L, ct, lt = rec(t, h)
            pV, pM, pU, p37 = T["pV" + h], T["pM" + h], T["pU" + h], T["p37" + h]
            tbn = "pUA" if h == "A" else "pMA"
            tb = T[tbn]
            o = H2 * hi
            sL, sC = "s%dL%s" % (t, h), "s%dC%s" % (t, h)
            for j in range(4):
                sl = slice(1536 * j, 1536 * j + 1536)
                V(768, SCAN(T["VS" + h][:, sl], T.m6[:], T["z" + h][:, sl], O.mult, O.max), tuple("z%d%s" % (k, h) for k in range(6)) + ("m6",), ("VS%d%s" % (j, h),))
            vt = tuple("VS%d%s" % (j, h) for j in range(4))
            for c, m0 in enumerate(range(NV[h], 16, 8)):
                ms = range(m0, min(16, m0 + 8))
                ps, bk = (p37, "p37" + h) if c == 0 else (pM, "pM" + h)
                mm = []
                for j, m in enumerate(ms):
                    mm += [MM(ps[:, 64 * j:64 * j + 64], T.idn[:], vm(h, m), True, False), MM(ps[:, 64 * j:64 * j + 64], T.nid[:], B("Fs" + h), False, True)]
                P(128 * len(ms), mm, vt + ("Fs" + h, "idn", "nid"), ("VF%d%s" % (c, h),), (bk,))
                S(64 * len(ms), ACT(T["ind" + h][:, 64 * m0:64 * (m0 + len(ms))], ps[:, 0:64 * len(ms)], AF.Sign, bias=T.half[:, 0:1]),
                  ("VF%d%s" % (c, h), "half0"), tuple("ind%d%s" % (m, h) for m in ms), (bk,))
            for m in range(NV[h]):
                V(64, TT(T["ind" + h][:, 64 * m:64 * m + 64], vm(h, m), pV[:, 448:512], O.is_ge), vt + ("F" + h,), ("ind%d%s" % (m, h),), ("pV" + h,))
            prev = ()
            for c in range(2):
                prev = (P(512, ([MM(pU[:, 0:64], B("kq" + h), T.ones[:, 0:64], True, False)] if c == 0 else [])
                          + [MM(pU[:, 0:64], T.Es[:, 128 * m:128 * m + 128], T["ind" + h][:, 64 * m:64 * m + 64], False, m == 15) for m in range(8 * c, 8 * c + 8)],
                          tuple("ind%d%s" % (m, h) for m in range(8 * c, 8 * c + 8)) + ("Es", "kq" + h, "ones"), ("cnt%d%s" % (c, h),), ("pU" + h,), after=prev),)
            V(64, TT(B("key" + h), pU[:, 0:64], B("Kp" + h), O.min), ("cnt0" + h, "cnt1" + h, "Kp" + h), ("key" + h,), ("pU" + h,))
            kb, acc = B("kb" + h), B("acc" + h)
            V(64, TURN(B("kt" + h), B("key" + h)), ("key" + h,), ("kt" + h,))
            V(64, SCAN(kb, T.m16[:], B("kt" + h), O.mult, O.max), ("kt" + h, "m16"), ("kb" + h,))
            for j in range(4):
                V(64, TS(B("aT" + h, 16 * j, 16 * j + 16), B("kt" + h, 16 * j, 16 * j + 16), B("kb" + h, 16 * j + 15, 16 * j + 16), None, O.is_equal),
                  ("kt" + h, "kb" + h), ("aT%d%s" % (j, h),))
            V(64, TURN(acc, B("aT" + h)), tuple("aT%d%s" % (j, h) for j in range(4)), ("acc" + h,))
            P(128, [MM(p37[:, 384:448], T.bm[:], acc, True, True), MM(p37[:, 448:512], T.ones[:], acc, True, True)],
              ("acc" + h, "bm", "ones"), ("okB" + h,), ("p37" + h,))
            AP = T["AP" + h]
            for k in range(1, 7):
                V(64, TT(AP[:, 64 * k:64 * k + 64], acc, pV[:, 64 * k - 64:64 * k], O.mult), ("acc" + h, "P%d%s" % (k, h)), ("AP%d%s" % (k, h),), ("pV" + h,))
            S(64, ACT(B("okS" + h), p37[:, 384:448], AF.Copy), ("okB" + h,), ("okS" + h,), ("p37" + h,))
            S(64, ACT(B("nok" + h), p37[:, 384:448], AF.Copy, scale=-1.0, bias=1.0), ("okB" + h,), ("nok" + h,), ("p37" + h,))
            if not last:
                V(64, lambda a_=B("asum" + h), b_=p37[:, 448:512]: g.vector.tensor_reduce(a_, b_, AxisListType.X, O.add), ("okB" + h,), ("asum" + h,), ("p37" + h,))
            apt = tuple("AP%d%s" % (k, h) for k in range(7))
            P(320, [MM(pU[:, 192:512], T.bm[:], AP[:, 64:384], True, True)], apt[1:6] + ("bm",), ("Pst" + h,), ("pU" + h,))
            P(768, [MM(p37[:, 0:384], T.bm[:], AP[:, 64:448], True, False), MM(p37[:, 0:384], T.nbm[:], AP[:, 0:384], False, True)],
              apt + ("bm", "nbm"), ("Nst" + h,), ("p37" + h,))
            V(64, TT(B("aL" + h), acc, pV[:, 384:448], O.mult), ("acc" + h, "L" + h), ("aL" + h,), ("pV" + h,))
            if EQS[h]:
                for k in range(1, 6):
                    S(64, ACT(T["SQ" + h][:, 64 * k - 64:64 * k], pU[:, 128 + 64 * k:192 + 64 * k], AF.Square, bias=T.nq[:, k:k + 1]),
                      ("Pst" + h, "nq"), ("SQ%d%s" % (k, h),), ("pU" + h,))
                S(320, ACT(T["EQ" + h][:, 64:384], T["SQ" + h][:], AF.Relu, scale=-1.0, bias=T.onec[:]), tuple("SQ%d%s" % (k, h) for k in range(1, 6)) + ("onec",),
                  tuple("EQ%d%s" % (k, h) for k in range(1, 6)))
            else:
                for k in range(1, 6):
                    V(64, TS(T["EQ" + h][:, 64 * k:64 * k + 64], pU[:, 128 + 64 * k:192 + 64 * k], T.qk[:, k:k + 1], None, O.is_equal),
                      ("Pst" + h, "qk%d" % k), ("EQ%d%s" % (k, h),), ("pU" + h,))
            V(384, TT(T["EN" + h][:], T["EQ" + h][:], p37[:, 0:384], O.mult), ("Nst" + h,) + tuple("EQ%d%s" % (k, h) for k in range(6)), ("EN" + h,), ("p37" + h,))
            V(64, TT(B("nokL" + h), B("nok" + h), pV[:, 384:448], O.mult), ("nok" + h, "L" + h), ("nokL" + h,), ("pV" + h,))
            P(512, [MM(p37[:, 384:448], T.idn[:], B("nokL" + h), True, False), MM(p37[:, 384:448], T.bm[:], acc, False, False)]
              + [MM(p37[:, 384:448], T.idn[:], T["EN" + h][:, 64 * k:64 * k + 64], False, k == 5) for k in range(6)],
              ("EN" + h, "nokL" + h, "acc" + h, "idn", "bm"), ("ls" + h,), ("p37" + h,))
            S(64, ACT(T[sL][:], p37[:, 384:448], AF.Copy), ("ls" + h,), (sL,), ("p37" + h,))
            if not last:
                send(sL, "in%dL%s" % (t + 1, h), "arr%dL%s" % (t + 1, h), 1, (sL,))
            else:
                dma("y", T.yl[:, o:o + H2], T[sL][:], (sL,), ())
            P(256, [MM(pM[:, 64 * l:64 * l + 64], T.hsh[:, 128 * l:128 * l + 128], C, True, True) for l in range(4)], (ct, "hsh"), ("SH" + h,), ("pM" + h,))
            P(64, [MM(pM[:, 320:384], T.tri[:], B("aL" + h), True, True)], ("aL" + h, "tri"), ("sh" + h,), ("pM" + h,))
            for l in range(1, 5):
                S(64, ACT(T["ES" + h][:, 64 * l - 64:64 * l], pM[:, 320:384], AF.Sign, bias=T.half[:, l:l + 1]), ("sh" + h, "half%d" % l), ("ES%d%s" % (l, h),), ("pM" + h,))
            V(256, TT(T["EC" + h][:], T["ES" + h][:], pM[:, 0:256], O.mult), ("SH" + h,) + tuple("ES%d%s" % (l, h) for l in range(1, 5)), ("EC" + h,), ("pM" + h,))
            P(384, [MM(pM[:, 384:448], T.hid[:, 0:128], C, True, False), MM(pM[:, 384:448], T.hid[:, 128:256], C, False, False)]
              + [MM(pM[:, 384:448], T.idn[:], T["EC" + h][:, 64 * l:64 * l + 64], False, l == 3) for l in range(4)],
              ("EC" + h, "idn", "hid0", "hid1", ct), ("cs" + h,), ("pM" + h,))
            S(64, ACT(T[sC][:], pM[:, 384:448], AF.Copy), ("cs" + h,), (sC,), ("pM" + h,))
            if not last:
                send(sC, "in%dC%s" % (t + 1, h), "arr%dC%s" % (t + 1, h), 1, (sC,))
            else:
                dma("y", T.yc[:, o:o + H2], T[sC][:], (sC,), ())
            S(64, ACT(B("aM" + h), acc, AF.Copy, scale=T.q6[:]), ("acc" + h, "q6"), ("aM" + h,))
            P(1024, [MM(tb[:, 0:8], T.Em[:, 128 * a:128 * a + 128], B("aM" + h, a, 128, 16), a == 0, a == 15) for a in range(16)],
              ("aM" + h, "acc" + h) + EM, ("tb" + h,), (tbn,))
            V(4, TT(T["voff" + h][:], tb[:, 0:4], B("Kv" + h), O.add), ("tb" + h, "Kv" + h), ("voff" + h,), (tbn,))
            V(4, CP(B("tt" + h), tb[:, 4:8]), ("tb" + h,), ("okd" + h,), (tbn,))
            add("s", 0.16, [lambda o_=B("Vsel" + h), v_=T["VS" + h], f_=T["voff" + h]: g.scalar.activation(o_, v_[:, 0:6144].indirect(f_[:, 0:4]), AF.Copy)],
                vt + ("voff" + h,), ("Vsel" + h,))
            P(1024, [MM(tb[:, 8:12], T.Wm[:, 128 * a:128 * a + 128], B("Vsel" + h, a, 64, 16), a == 0, a == 15) for a in range(16)],
              ("Vsel" + h,) + WM, ("hd" + h,), (tbn,))
            V(4, CP(B("h0" + h), tb[:, 8:12]), ("hd" + h,), ("h0" + h,), (tbn,))
            V(4, TS(B("h1" + h), B("h0" + h), 31, None, O.bitwise_and), ("h0" + h,), ("h1" + h,))
            V(4, TT(B("h2" + h), B("h1" + h), B("K1" + h), O.add), ("h1" + h, "K1" + h), ("h2" + h,))
            V(4, TT(B("h3" + h), B("h2" + h), B("tt" + h), O.mult), ("h2" + h, "okd" + h), ("h3" + h,))
            V(4, TT(T["toff" + h][:], B("h3" + h), B("K2" + h), O.add), ("h3" + h, "K2" + h), ("toff" + h,))
            if not last:
                add("v", 0.25, [lambda f_=T["toff" + h], i_=B("Vsel" + h): g.vector.tensor_copy(T.X[:, 0:4224].indirect(f_[:, 0:4]), i_)],
                    ("toff" + h, "Vsel" + h, "Xd"), ("X",))
            else:
                add("s", 0.16, [lambda o_=B("xo" + h), f_=T["toff" + h]: g.scalar.activation(o_, T.X[:, 0:4224].indirect(f_[:, 0:4]), AF.Copy)],
                    ("X", "Xd", "toff" + h), ("xo" + h,))
                V(128, TT(B("xd" + h), B("Vsel" + h), B("xo" + h), O.subtract), ("Vsel" + h, "xo" + h), ("xd" + h,))
                V(128, TT(B("xe" + h), B("xd" + h), B("okS" + h), O.mult), ("xd" + h, "okS" + h), ("xe" + h,))
                V(128, TT(B("yss" + h), B("xe" + h), B("S0" + h), O.add), ("xe" + h, "S0" + h), ("yss" + h,))
                dma("s", T.ys[:, o:o + H2], B("yss" + h), ("yss" + h,), ())
            Fp = pV[:, 448:512]
            V(64, TT(B("fd" + h), B("Vsel" + h), Fp, O.subtract), ("Vsel" + h, "F" + h), ("fd" + h,), ("pV" + h,))
            V(128, TT(B("xd" + h), B("fd" + h), B("okS" + h), O.mult), ("fd" + h, "okS" + h), ("xd" + h,))
            V(64, TS(B("fi" + h), B("xd" + h), 0.5, -0.25, O.mult, O.add), ("xd" + h,), ("fi" + h,))
            if not last:
                V(64, TT(B("Fs" + h), B("fi" + h), Fp, O.add), ("fi" + h, "F" + h), ("Fs" + h,), ("pV" + h,))
                V(64, TT(Fp, B("fi" + h), Fp, O.add), ("fi" + h, "F" + h), ("F" + h,), ("pV" + h,))
            else:
                V(64, TT(B("yfs" + h), B("fi" + h), Fp, O.add), ("fi" + h, "F" + h), ("yfs" + h,), ("pV" + h,))
                dma("s", T.yf[:, o:o + H2], B("yfs" + h), ("yfs" + h,), ())

    n = len(ops)
    succ = [[] for _ in range(n)]
    for k, p in enumerate(ops):
        for d in p["all"]:
            succ[d].append(k)
    prio = [0.0] * n
    for k in range(n - 1, -1, -1):
        prio[k] = ops[k]["cost"] + 0.1 + max([prio[s] for s in succ[k]], default=0.0)
    left = [len(p["all"]) for p in ops]
    ready = [0.0] * n
    free, pool, order = {}, {}, []
    for k in range(n):
        if left[k] == 0:
            pool.setdefault(ops[k]["q"], []).append(k)
    while len(order) < n:
        best = None
        for q, lst in pool.items():
            if lst:
                s0 = max(free.get(q, 0.0) if q != "r" else 0.0, min(ready[k] for k in lst))
                if best is None or s0 < best[0]:
                    best = (s0, q)
        s0, q = best
        k = max((k for k in pool[q] if ready[k] <= s0 + 0.02), key=lambda k: prio[k])
        s0 = max(s0, ready[k])
        pool[q].remove(k)
        order.append(k)
        hold = 0.1 if (ops[k]["sem"] is not None and q != "r") else ops[k]["cost"]
        free[q] = s0 + hold
        end = s0 + ops[k]["cost"]
        for s in succ[k]:
            ready[s] = max(ready[s], end + (0.15 if ops[s]["q"] == q else 0.25))
            left[s] -= 1
            if left[s] == 0:
                pool.setdefault(ops[s]["q"], []).append(s)
    count = {q: 0 for q in qsem}
    know = {q: {} for q in eng}
    done, seen = {}, {}
    for k in order:
        p = ops[k]
        q = p["q"]
        if q == "r":
            done[k], seen[k] = p["sem"], {}
            continue
        need, via = {}, {}
        for d in p["deps"]:
            if done[d] is None:
                continue
            s, v = done[d]
            if know[q].get(s, 0) < v:
                need[s] = max(need.get(s, 0), v)
                for s2, v2 in seen[d].items():
                    via[s2] = max(via.get(s2, 0), v2)
        for s, v in need.items():
            eng[q].wait_ge(T.sem[s], v)
            know[q][s] = max(know[q].get(s, 0), v)
        for s, v in via.items():
            know[q][s] = max(know[q].get(s, 0), v)
        seen[k] = dict(know[q])
        if p["sem"] is not None:
            s, v = p["sem"]
            ins = p["fns"][0]()
            if v is None:
                done[k] = None
            else:
                ins.then_inc(T.sem[s], v)
                done[k] = (s, v)
        else:
            for f in p["fns"]:
                f().then_inc(T.sem[qsem[q]], 1)
                count[q] += 1
            done[k] = (qsem[q], count[q])
    for q, s in qsem.items():
        g.wait_ge(T.sem[s], count[q])
    for j in range(ndma[0]):
        g.wait_ge(T.sem["d%d" % j], 16)
    for p in ops:
        if p["q"] == "r":
            g.wait_ge(T.sem[p["sem"][0]], p["sem"][1])
    g.wait_ge(T.sem.loc, loc[0])
